import numpy as np
import ml_dtypes


def mxq(x, axis, fmt="e4m3"):
    dtype, down = {"e4m3": (ml_dtypes.float8_e4m3fn, 7), "e5m2": (ml_dtypes.float8_e5m2, 14)}[fmt]
    v = np.moveaxis(np.asarray(x, np.float32).astype(ml_dtypes.bfloat16).astype(np.float64), axis, -1)
    blocks = v.reshape(v.shape[:-1] + (-1, 32))
    amax = np.abs(blocks).max(-1, keepdims=True)
    byte = np.maximum(np.where(amax > 0, np.frexp(amax)[1] - 1 + 127, 0) - down, 1)
    scale = np.exp2(byte - 127.0)
    codes = (blocks / scale).astype(np.float32).astype(dtype).astype(np.float64)
    return np.moveaxis((codes * scale).reshape(v.shape), -1, axis)


WIDE = False


def mx_kscale(k):
    if not WIDE:
        return np.ones(k)
    levels = np.array([10, -10, 5, -5, 0])
    if k % 512:
        return np.exp2(np.random.permutation(np.resize(levels, k // 32))).repeat(32)
    a = np.empty((k // 512, 16))
    for p in range(k // 512):
        a[p, :8] = np.random.permutation(np.resize(levels, 8))
        for g in range(8):
            far = levels[np.abs(levels - a[p, g]) >= 10]
            a[p, g + 8] = far[np.random.randint(len(far))]
    return np.exp2(a.ravel()).repeat(32)


def f64(x):
    return np.asarray(x).astype(np.float64)


def striped(idx):
    return np.tile(idx.reshape(-1, 16).T, (8, 1)).astype(np.uint16)


def unstriped(offs):
    return offs[:16].T.reshape(-1).astype(np.int64)


def pack_weight(w):
    k, n = w.shape
    w = f64(np.asarray(w, np.float32).astype(ml_dtypes.bfloat16)).reshape(k // 32, 32, n)
    amax = np.abs(w).max(1)
    byte = np.clip(np.where(amax > 0, np.frexp(amax)[1] - 1 + 127 - 7, 1), 1, 254)
    scaled = (w * np.exp2(127.0 - byte)[:, None, :]).reshape(k, n).astype(np.float32)
    words = np.ascontiguousarray(scaled.reshape(k // 512, 128, 4, n).transpose(0, 1, 3, 2)).astype(ml_dtypes.float8_e4m3fn).view(np.uint8)
    return words, np.ascontiguousarray(byte.astype(np.uint8).reshape(k // 512, 16, n))


def unpack_weight(words, scales):
    g, p, n, _ = words.shape
    vals = np.ascontiguousarray(words).view(ml_dtypes.float8_e4m3fn).astype(np.float64) * np.repeat(np.exp2(scales.astype(np.float64) - 127.0), 8, axis=1)[..., None]
    return vals.transpose(0, 1, 3, 2).reshape(g * 512, n)


def gelu(v):
    return 0.5 * v * (1.0 + np.tanh(np.sqrt(2.0 / np.pi) * (v + 0.044715 * v**3)))

def planes(y):
    n, m = y.shape
    v = y.astype(np.float32).astype(ml_dtypes.bfloat16).astype(np.float64).reshape(n // 32, 32, m)
    top = np.abs(v).max(1)
    byte = np.clip(np.where(top > 0, np.frexp(top)[1] - 1 + 127 - 7, 1), 1, 254)
    codes = (v * np.exp2(127.0 - byte)[:, None, :]).reshape(n, m).astype(np.float32).astype(ml_dtypes.float8_e4m3fn).view(np.uint8)
    words = codes.reshape(n // 512, 128, 4, m).transpose(0, 1, 3, 2)
    return np.ascontiguousarray(words), np.ascontiguousarray(byte.astype(np.uint8).reshape(n // 512, 16, m))


K, T, N = 512, 512, 512
P = 2 ** 7


def setup_inputs():
    n = np.random.standard_normal
    s = mx_kscale(K)[:, None]
    packed_xT = pack_weight(n((K, T)) * s)
    return {
        "x_words": packed_xT[0],
        "x_scales": packed_xT[1],
        "w1": (n((K, N)) / np.sqrt(K) / s).astype(np.float32),
        "frac": np.tile(np.random.uniform(0.05, 0.95, T), (P, 1)).astype(np.float32),
        "left": striped(np.random.permutation(T)),
        "right": striped(np.random.permutation(T)),
    }


def reference(x_words, x_scales, w1, frac, left, right):
    xq = unpack_weight(x_words, x_scales)
    y = gelu(mxq(f64(w1), 0, "e4m3").T @ xq)
    l = y[:, unstriped(left)]
    out_0 = l + (y[:, unstriped(right)] - l) * f64(frac)[:1]
    return (out_0,) + planes(out_0)

@@ -1,0 +1,173 @@
+from contextlib import ExitStack
+
+import concourse.mybir as mybir
+from concourse.masks import make_identity
+
+K, T, N = 512, 512, 512
+FLOPS = 2 * K * T * N
+
+F32 = mybir.dt.float32
+BF16 = mybir.dt.bfloat16
+I32 = mybir.dt.int32
+U32 = mybir.dt.uint32
+U16 = mybir.dt.uint16
+U8 = mybir.dt.uint8
+FP8X4 = mybir.dt.float8_e4m3fn_x4
+ALU = mybir.AluOpType
+ACT = mybir.ActivationFunctionType
+
+P = 128
+PACK = 4
+STRIPE = 16
+CHUNKS = (256, 128, 128)
+ON_TENSOR = 0
+
+
+def tile_picked_wlerp_gelu_lo_kernel(
+    tc, x_words, x_scales, w1, frac, left, right, out_0, out_1, out_2
+):
+    nc = tc.nc
+    with ExitStack() as ctx:
+        keep = ctx.enter_context(tc.tile_pool(name="keep", bufs=1))
+        psum = ctx.enter_context(tc.psum_pool(name="psum", bufs=1))
+
+        w_rows = w1.rearrange("(p j) m -> p j m", j=PACK)
+        w_raw = [keep.tile([P, 2, N], F32, name=f"w_raw{h}", align_bytes=64) for h in range(2)]
+        for h in range(2):
+            nc.sync.dma_start(out=w_raw[h][:], in_=w_rows[:, 2 * h : 2 * h + 2, :])
+
+        x_codes = keep.tile([P, T], U32, name="x_codes", align_bytes=64)
+        nc.sync.dma_start(
+            out=x_codes[:].bitcast(I32),
+            in_=x_words[0].rearrange("p n t -> p (n t)").bitcast(I32),
+        )
+        x_scale = keep.tile([P, T], U8, name="x_scale", align_bytes=64)
+        nc.gpsimd.memset(x_scale[:].bitcast(U32), 0)
+        for q in range(4):
+            queue = nc.scalar if q < 2 else nc.gpsimd
+            queue.dma_start(
+                out=x_scale[32 * q : 32 * q + 4, :].bitcast(I32),
+                in_=x_scales[0, 4 * q : 4 * q + 4, :].bitcast(I32),
+            )
+        right_offs = keep.tile([P, T // STRIPE], U16, name="right_offs")
+        nc.sync.dma_start(right_offs[:], right)
+        left_offs = keep.tile([P, T // STRIPE], U16, name="left_offs")
+        nc.sync.dma_start(left_offs[:], left)
+        f_right = keep.tile([P, T], F32, name="f_right", align_bytes=64)
+        nc.sync.dma_start(out=f_right[:], in_=frac)
+        ident = None
+
+        w_bf = keep.tile([P, PACK, P, PACK], BF16, name="w_bf", align_bytes=64)
+        w_codes = keep.tile([P, N], U32, name="w_codes", align_bytes=64)
+        w_scale = keep.tile([P, N], U8, name="w_scale", align_bytes=64)
+
+        def round_w(copy, h, t0, t1):
+            copy(
+                out=w_bf[:, t0:t1, :, 2 * h : 2 * h + 2].rearrange("p t m j -> p m t j"),
+                in_=w_raw[h][:].rearrange("p j (m t) -> p m t j", t=PACK)[:, :, t0:t1, :],
+            )
+
+        def quantize_w(t0, t1):
+            nc.vector.quantize_mx(
+                out=w_codes[:, t0 * P : t1 * P].bitcast(FP8X4),
+                scales=w_scale[:, t0 * P : t1 * P],
+                in_=w_bf[:, t0:t1].rearrange("p t m j -> p (t m j)"),
+            )
+
+        y = [keep.tile([P, T], F32, name=f"y{t}", align_bytes=64) for t in range(PACK)]
+
+        def project(t, c0, c1):
+            acc = psum.tile([P, c1 - c0], F32, name="acc", bufs=5)
+            nc.tensor.matmul_mx(
+                out=acc[:],
+                lhsT=w_codes[:, t * P : (t + 1) * P].bitcast(FP8X4),
+                lhsT_scale=w_scale[:, t * P : (t + 1) * P],
+                rhs=x_codes[:, c0:c1].bitcast(FP8X4),
+                rhs_scale=x_scale[:, c0:c1],
+                start=True,
+                stop=True,
+            )
+            nc.scalar.activation(y[t][:, c0:c1], acc[:], ACT.Gelu_apprx_tanh)
+
+        round_w(nc.vector.tensor_copy, 0, 0, PACK)
+        round_w(nc.vector.tensor_copy, 1, 0, 1)
+        quantize_w(0, 1)
+        project(0, 0, T // 2)
+        project(0, T // 2, T)
+        round_w(nc.vector.tensor_copy, 1, 1, 2)
+        quantize_w(1, 2)
+        project(1, 0, T)
+        round_w(nc.vector.tensor_copy, 1, 2, PACK)
+        quantize_w(2, 4)
+        project(2, 0, T)
+        project(3, 0, T)
+        f_left = keep.tile([P, T], F32, name="f_left", align_bytes=64)
+        nc.vector.tensor_scalar(f_left[:], f_right[:], -1.0, 1.0, ALU.mult, ALU.add)
+
+        out_rows = out_0.rearrange("(p t) v -> p t v", t=PACK)
+        out_words = out_1[0].rearrange("p n t -> p (n t)").bitcast(I32)
+        o_scale = keep.tile([P, T], U8, name="o_scale", align_bytes=64)
+
+        def quantize_out(o_bf, v0, v1):
+            o_codes = keep.tile([P, v1 - v0], U32, name=f"o_codes{v0}", align_bytes=64)
+            nc.vector.quantize_mx(
+                out=o_codes[:].bitcast(FP8X4),
+                scales=o_scale[:, v0:v1],
+                in_=o_bf[:].rearrange("p v t -> p (v t)"),
+            )
+            nc.sync.dma_start(out=out_words[:, v0:v1], in_=o_codes[:].bitcast(I32))
+
+        def add_on_tensor(from_r, from_l, u0, v0):
+            turned = psum.tile([P, PACK, P], F32, name="turned", bufs=1)
+            for t in range(PACK):
+                nc.tensor.matmul(turned[:, t, :], from_r[:, t, u0 : u0 + P], ident[:], start=True, stop=False, is_transpose=True)
+                nc.tensor.matmul(turned[:, t, :], from_l[:, t, u0 : u0 + P], ident[:], start=False, stop=True, is_transpose=True)
+            turned_sb = keep.tile([P, PACK, P], F32, name=f"turned_sb{v0}", align_bytes=64)
+            nc.scalar.copy(out=turned_sb[:], in_=turned[:])
+            back = psum.tile([P, PACK, P], F32, name="back", bufs=2)
+            for t in range(PACK):
+                nc.tensor.transpose(back[:, t, :], turned_sb[:, t, :], ident[:])
+            o_bf = keep.tile([P, P, PACK], BF16, name=f"o_bf{v0}", align_bytes=64)
+            nc.scalar.copy(out=o_bf[:], in_=back[:].rearrange("p t v -> p v t"))
+            o = keep.tile([P, PACK, P], F32, name=f"o{v0}", align_bytes=64)
+            nc.scalar.copy(out=o[:], in_=back[:])
+            nc.sync.dma_start(out=out_rows[:, :, v0 : v0 + P], in_=o[:])
+            quantize_out(o_bf, v0, v0 + P)
+
+        def add_on_vector(from_r, from_l, v0, v1):
+            o = keep.tile([P, PACK, v1 - v0], F32, name=f"o{v0}", align_bytes=64)
+            nc.vector.tensor_tensor(o[:], from_r[:], from_l[:], ALU.add)
+            nc.sync.dma_start(out=out_rows[:, :, v0:v1], in_=o[:])
+            o_bf = keep.tile([P, v1 - v0, PACK], BF16, name=f"o_bf{v0}", align_bytes=64)
+            copy = nc.vector.tensor_copy if v1 == T else nc.scalar.copy
+            copy(
+                out=o_bf[:].rearrange("p (c i) t -> p c t i", i=4),
+                in_=o[:].rearrange("p t (c i) -> p c t i", i=4),
+            )
+            quantize_out(o_bf, v0, v1)
+
+        v0 = 0
+        for c, width in enumerate(CHUNKS):
+            v1 = v0 + width
+            cols = slice(v0 // STRIPE, v1 // STRIPE)
+            from_r = keep.tile([P, PACK, width], F32, name=f"from_r{c}", align_bytes=64)
+            from_l = keep.tile([P, PACK, width], F32, name=f"from_l{c}", align_bytes=64)
+            for t in range(PACK):
+                nc.vector.tensor_tensor(
+                    from_r[:, t, :], y[t][:].indirect(right_offs[:, cols]), f_right[:, v0:v1], ALU.mult
+                )
+                nc.vector.tensor_tensor(
+                    from_l[:, t, :], y[t][:].indirect(left_offs[:, cols]), f_left[:, v0:v1], ALU.mult
+                )
+            if v1 <= ON_TENSOR:
+                for u0 in range(0, width, P):
+                    add_on_tensor(from_r, from_l, u0, v0 + u0)
+            else:
+                add_on_vector(from_r, from_l, v0, v1)
+            v0 = v1
+        for q in range(4):
+            queue = nc.scalar if q % 2 else nc.sync
+            queue.dma_start(
+                out=out_2[0, 4 * q : 4 * q + 4, :].bitcast(I32),
+                in_=o_scale[32 * q : 32 * q + 4, :].bitcast(I32),
+            )

@@ -19,8 +19,9 @@ ACT = mybir.ActivationFunctionType
 P = 128
 PACK = 4
 STRIPE = 16
-CHUNKS = (256, 128, 128)
-ON_TENSOR = 0
+CHUNKS = (128, 128, 128, 128)
+ON_TENSOR = 384
+RING = 13
 
 
 def tile_picked_wlerp_gelu_lo_kernel(
@@ -36,26 +37,26 @@ def tile_picked_wlerp_gelu_lo_kernel(
         for h in range(2):
             nc.sync.dma_start(out=w_raw[h][:], in_=w_rows[:, 2 * h : 2 * h + 2, :])
 
+        x_scale = keep.tile([P, T], U8, name="x_scale", align_bytes=64)
+        nc.vector.memset(x_scale[:].bitcast(U32), 0)
+        for q in range(4):
+            nc.scalar.dma_start(
+                out=x_scale[32 * q : 32 * q + 4, :].bitcast(I32),
+                in_=x_scales[0, 4 * q : 4 * q + 4, :].bitcast(I32),
+            )
         x_codes = keep.tile([P, T], U32, name="x_codes", align_bytes=64)
         nc.sync.dma_start(
             out=x_codes[:].bitcast(I32),
             in_=x_words[0].rearrange("p n t -> p (n t)").bitcast(I32),
         )
-        x_scale = keep.tile([P, T], U8, name="x_scale", align_bytes=64)
-        nc.gpsimd.memset(x_scale[:].bitcast(U32), 0)
-        for q in range(4):
-            queue = nc.scalar if q < 2 else nc.gpsimd
-            queue.dma_start(
-                out=x_scale[32 * q : 32 * q + 4, :].bitcast(I32),
-                in_=x_scales[0, 4 * q : 4 * q + 4, :].bitcast(I32),
-            )
+        f_right = keep.tile([P, T], F32, name="f_right", align_bytes=64)
+        nc.sync.dma_start(out=f_right[:], in_=frac)
         right_offs = keep.tile([P, T // STRIPE], U16, name="right_offs")
         nc.sync.dma_start(right_offs[:], right)
         left_offs = keep.tile([P, T // STRIPE], U16, name="left_offs")
         nc.sync.dma_start(left_offs[:], left)
-        f_right = keep.tile([P, T], F32, name="f_right", align_bytes=64)
-        nc.sync.dma_start(out=f_right[:], in_=frac)
-        ident = None
+        ident = keep.tile([P, P], F32, name="ident", align_bytes=64)
+        make_identity(nc, ident[:])
 
         w_bf = keep.tile([P, PACK, P, PACK], BF16, name="w_bf", align_bytes=64)
         w_codes = keep.tile([P, N], U32, name="w_codes", align_bytes=64)
@@ -77,7 +78,7 @@ def tile_picked_wlerp_gelu_lo_kernel(
         y = [keep.tile([P, T], F32, name=f"y{t}", align_bytes=64) for t in range(PACK)]
 
         def project(t, c0, c1):
-            acc = psum.tile([P, c1 - c0], F32, name="acc", bufs=5)
+            acc = psum.tile([P, c1 - c0], F32, name="acc", bufs=4)
             nc.tensor.matmul_mx(
                 out=acc[:],
                 lhsT=w_codes[:, t * P : (t + 1) * P].bitcast(FP8X4),
@@ -108,63 +109,68 @@ def tile_picked_wlerp_gelu_lo_kernel(
         out_words = out_1[0].rearrange("p n t -> p (n t)").bitcast(I32)
         o_scale = keep.tile([P, T], U8, name="o_scale", align_bytes=64)
 
-        def quantize_out(o_bf, v0, v1):
-            o_codes = keep.tile([P, v1 - v0], U32, name=f"o_codes{v0}", align_bytes=64)
-            nc.vector.quantize_mx(
-                out=o_codes[:].bitcast(FP8X4),
-                scales=o_scale[:, v0:v1],
-                in_=o_bf[:].rearrange("p v t -> p (v t)"),
-            )
-            nc.sync.dma_start(out=out_words[:, v0:v1], in_=o_codes[:].bitcast(I32))
+        o_bf = keep.tile([P, T, PACK], BF16, name="o_bf", align_bytes=64)
+        o_codes = keep.tile([P, T], U32, name="o_codes", align_bytes=64)
 
-        def add_on_tensor(from_r, from_l, u0, v0):
-            turned = psum.tile([P, PACK, P], F32, name="turned", bufs=1)
+        def quantize_out(v0, v1):
+            nc.vector.quantize_mx(
+                out=o_codes[:, v0:v1].bitcast(FP8X4),
+                scales=o_scale[:, v0:v1],
+                in_=o_bf[:, v0:v1, :].rearrange("p v t -> p (v t)"),
+            )
+
+        def store_codes(v0, v1):
+            nc.sync.dma_start(out=out_words[:, v0:v1], in_=o_codes[:, v0:v1].bitcast(I32))
+
+        def gather(dst_r, dst_l, t, v0, v1):
+            cols = slice(v0 // STRIPE, v1 // STRIPE)
+            nc.vector.tensor_tensor(dst_r, y[t][:].indirect(right_offs[:, cols]), f_right[:, v0:v1], ALU.mult)
+            nc.vector.tensor_tensor(dst_l, y[t][:].indirect(left_offs[:, cols]), f_left[:, v0:v1], ALU.mult)
+
+        def add_on_tensor(v0):
+            turned = psum.tile([P, PACK, P], F32, name="turned", bufs=2)
             for t in range(PACK):
-                nc.tensor.matmul(turned[:, t, :], from_r[:, t, u0 : u0 + P], ident[:], start=True, stop=False, is_transpose=True)
-                nc.tensor.matmul(turned[:, t, :], from_l[:, t, u0 : u0 + P], ident[:], start=False, stop=True, is_transpose=True)
+                terms = keep.tile([P, 2, P], F32, name="terms", bufs=RING, align_bytes=64)
+                gather(terms[:, 0, :], terms[:, 1, :], t, v0, v0 + P)
+                nc.tensor.matmul(turned[:, t, :], terms[:, 0, :], ident[:], start=True, stop=False, is_transpose=True)
+                nc.tensor.matmul(turned[:, t, :], terms[:, 1, :], ident[:], start=False, stop=True, is_transpose=True)
             turned_sb = keep.tile([P, PACK, P], F32, name=f"turned_sb{v0}", align_bytes=64)
             nc.scalar.copy(out=turned_sb[:], in_=turned[:])
             back = psum.tile([P, PACK, P], F32, name="back", bufs=2)
             for t in range(PACK):
                 nc.tensor.transpose(back[:, t, :], turned_sb[:, t, :], ident[:])
-            o_bf = keep.tile([P, P, PACK], BF16, name=f"o_bf{v0}", align_bytes=64)
-            nc.scalar.copy(out=o_bf[:], in_=back[:].rearrange("p t v -> p v t"))
+            nc.scalar.copy(out=o_bf[:, v0 : v0 + P, :], in_=back[:].rearrange("p t v -> p v t"))
             o = keep.tile([P, PACK, P], F32, name=f"o{v0}", align_bytes=64)
             nc.scalar.copy(out=o[:], in_=back[:])
-            nc.sync.dma_start(out=out_rows[:, :, v0 : v0 + P], in_=o[:])
-            quantize_out(o_bf, v0, v0 + P)
+            nc.scalar.dma_start(out=out_rows[:, :, v0 : v0 + P], in_=o[:])
 
-        def add_on_vector(from_r, from_l, v0, v1):
+        def add_on_vector(v0, v1):
+            terms = keep.tile([P, 2, PACK, v1 - v0], F32, name="terms", bufs=RING, align_bytes=64)
+            for t in range(PACK):
+                gather(terms[:, 0, t, :], terms[:, 1, t, :], t, v0, v1)
             o = keep.tile([P, PACK, v1 - v0], F32, name=f"o{v0}", align_bytes=64)
-            nc.vector.tensor_tensor(o[:], from_r[:], from_l[:], ALU.add)
+            nc.vector.tensor_tensor(o[:], terms[:, 0], terms[:, 1], ALU.add)
             nc.sync.dma_start(out=out_rows[:, :, v0:v1], in_=o[:])
-            o_bf = keep.tile([P, v1 - v0, PACK], BF16, name=f"o_bf{v0}", align_bytes=64)
             copy = nc.vector.tensor_copy if v1 == T else nc.scalar.copy
             copy(
-                out=o_bf[:].rearrange("p (c i) t -> p c t i", i=4),
+                out=o_bf[:, v0:v1, :].rearrange("p (c i) t -> p c t i", i=4),
                 in_=o[:].rearrange("p t (c i) -> p c t i", i=4),
             )
-            quantize_out(o_bf, v0, v1)
 
         v0 = 0
         for c, width in enumerate(CHUNKS):
             v1 = v0 + width
-            cols = slice(v0 // STRIPE, v1 // STRIPE)
-            from_r = keep.tile([P, PACK, width], F32, name=f"from_r{c}", align_bytes=64)
-            from_l = keep.tile([P, PACK, width], F32, name=f"from_l{c}", align_bytes=64)
-            for t in range(PACK):
-                nc.vector.tensor_tensor(
-                    from_r[:, t, :], y[t][:].indirect(right_offs[:, cols]), f_right[:, v0:v1], ALU.mult
-                )
-                nc.vector.tensor_tensor(
-                    from_l[:, t, :], y[t][:].indirect(left_offs[:, cols]), f_left[:, v0:v1], ALU.mult
-                )
             if v1 <= ON_TENSOR:
-                for u0 in range(0, width, P):
-                    add_on_tensor(from_r, from_l, u0, v0 + u0)
+                add_on_tensor(v0)
             else:
-                add_on_vector(from_r, from_l, v0, v1)
+                add_on_vector(v0, v1)
+            if v1 == T // 2:
+                quantize_out(0, v1)
+                store_codes(0, v1)
+            elif v1 > T // 2:
+                quantize_out(v0, v1)
             v0 = v1
+        store_codes(T // 2, T)
         for q in range(4):
             queue = nc.scalar if q % 2 else nc.sync
             queue.dma_start(

@@ -37,24 +37,25 @@ def tile_picked_wlerp_gelu_lo_kernel(
         for h in range(2):
             nc.sync.dma_start(out=w_raw[h][:], in_=w_rows[:, 2 * h : 2 * h + 2, :])
 
-        x_scale = keep.tile([P, T], U8, name="x_scale", align_bytes=64)
-        nc.vector.memset(x_scale[:].bitcast(U32), 0)
-        for q in range(4):
-            nc.scalar.dma_start(
-                out=x_scale[32 * q : 32 * q + 4, :].bitcast(I32),
-                in_=x_scales[0, 4 * q : 4 * q + 4, :].bitcast(I32),
-            )
         x_codes = keep.tile([P, T], U32, name="x_codes", align_bytes=64)
         nc.sync.dma_start(
             out=x_codes[:].bitcast(I32),
             in_=x_words[0].rearrange("p n t -> p (n t)").bitcast(I32),
         )
-        f_right = keep.tile([P, T], F32, name="f_right", align_bytes=64)
-        nc.sync.dma_start(out=f_right[:], in_=frac)
+        x_scale = keep.tile([P, T], U8, name="x_scale", align_bytes=64)
+        nc.gpsimd.memset(x_scale[:].bitcast(U32), 0)
+        for q in range(4):
+            queue = nc.scalar if q < 2 else nc.gpsimd
+            queue.dma_start(
+                out=x_scale[32 * q : 32 * q + 4, :].bitcast(I32),
+                in_=x_scales[0, 4 * q : 4 * q + 4, :].bitcast(I32),
+            )
         right_offs = keep.tile([P, T // STRIPE], U16, name="right_offs")
         nc.sync.dma_start(right_offs[:], right)
         left_offs = keep.tile([P, T // STRIPE], U16, name="left_offs")
         nc.sync.dma_start(left_offs[:], left)
+        f_right = keep.tile([P, T], F32, name="f_right", align_bytes=64)
+        nc.sync.dma_start(out=f_right[:], in_=frac)
         ident = keep.tile([P, P], F32, name="ident", align_bytes=64)
         make_identity(nc, ident[:])
 
@@ -134,21 +135,21 @@ def tile_picked_wlerp_gelu_lo_kernel(
                 gather(terms[:, 0, :], terms[:, 1, :], t, v0, v0 + P)
                 nc.tensor.matmul(turned[:, t, :], terms[:, 0, :], ident[:], start=True, stop=False, is_transpose=True)
                 nc.tensor.matmul(turned[:, t, :], terms[:, 1, :], ident[:], start=False, stop=True, is_transpose=True)
-            turned_sb = keep.tile([P, PACK, P], F32, name=f"turned_sb{v0}", align_bytes=64)
+            turned_sb = keep.tile([P, PACK, P], F32, name=f"staging{v0}", align_bytes=64)
             nc.scalar.copy(out=turned_sb[:], in_=turned[:])
             back = psum.tile([P, PACK, P], F32, name="back", bufs=2)
             for t in range(PACK):
                 nc.tensor.transpose(back[:, t, :], turned_sb[:, t, :], ident[:])
-            nc.scalar.copy(out=o_bf[:, v0 : v0 + P, :], in_=back[:].rearrange("p t v -> p v t"))
             o = keep.tile([P, PACK, P], F32, name=f"o{v0}", align_bytes=64)
             nc.scalar.copy(out=o[:], in_=back[:])
-            nc.scalar.dma_start(out=out_rows[:, :, v0 : v0 + P], in_=o[:])
+            nc.sync.dma_start(out=out_rows[:, :, v0 : v0 + P], in_=o[:])
+            nc.scalar.copy(out=o_bf[:, v0 : v0 + P, :], in_=back[:].rearrange("p t v -> p v t"))
 
         def add_on_vector(v0, v1):
             terms = keep.tile([P, 2, PACK, v1 - v0], F32, name="terms", bufs=RING, align_bytes=64)
             for t in range(PACK):
                 gather(terms[:, 0, t, :], terms[:, 1, t, :], t, v0, v1)
-            o = keep.tile([P, PACK, v1 - v0], F32, name=f"o{v0}", align_bytes=64)
+            o = keep.tile([P, PACK, v1 - v0], F32, name=f"staging{v0 - P}", align_bytes=64)
             nc.vector.tensor_tensor(o[:], terms[:, 0], terms[:, 1], ALU.add)
             nc.sync.dma_start(out=out_rows[:, :, v0:v1], in_=o[:])
             copy = nc.vector.tensor_copy if v1 == T else nc.scalar.copy

@@ -19,9 +19,8 @@ ACT = mybir.ActivationFunctionType
 P = 128
 PACK = 4
 STRIPE = 16
-CHUNKS = (128, 128, 128, 128)
-ON_TENSOR = 384
-RING = 13
+HALF = T // 2
+SPARE = 16
 
 
 def tile_picked_wlerp_gelu_lo_kernel(
@@ -32,6 +31,10 @@ def tile_picked_wlerp_gelu_lo_kernel(
         keep = ctx.enter_context(tc.tile_pool(name="keep", bufs=1))
         psum = ctx.enter_context(tc.psum_pool(name="psum", bufs=1))
 
+        right_offs = keep.tile([P, T // STRIPE], U16, name="right_offs")
+        nc.sync.dma_start(right_offs[:], right)
+        left_offs = keep.tile([P, T // STRIPE], U16, name="left_offs")
+        nc.sync.dma_start(left_offs[:], left)
         w_rows = w1.rearrange("(p j) m -> p j m", j=PACK)
         w_raw = [keep.tile([P, 2, N], F32, name=f"w_raw{h}", align_bytes=64) for h in range(2)]
         for h in range(2):
@@ -43,40 +46,41 @@ def tile_picked_wlerp_gelu_lo_kernel(
             in_=x_words[0].rearrange("p n t -> p (n t)").bitcast(I32),
         )
         x_scale = keep.tile([P, T], U8, name="x_scale", align_bytes=64)
-        nc.gpsimd.memset(x_scale[:].bitcast(U32), 0)
+        nc.vector.memset(x_scale[:].bitcast(U32), 0)
         for q in range(4):
-            queue = nc.scalar if q < 2 else nc.gpsimd
-            queue.dma_start(
+            nc.scalar.dma_start(
                 out=x_scale[32 * q : 32 * q + 4, :].bitcast(I32),
                 in_=x_scales[0, 4 * q : 4 * q + 4, :].bitcast(I32),
             )
-        right_offs = keep.tile([P, T // STRIPE], U16, name="right_offs")
-        nc.sync.dma_start(right_offs[:], right)
-        left_offs = keep.tile([P, T // STRIPE], U16, name="left_offs")
-        nc.sync.dma_start(left_offs[:], left)
         f_right = keep.tile([P, T], F32, name="f_right", align_bytes=64)
         nc.sync.dma_start(out=f_right[:], in_=frac)
         ident = keep.tile([P, P], F32, name="ident", align_bytes=64)
         make_identity(nc, ident[:])
 
-        w_bf = keep.tile([P, PACK, P, PACK], BF16, name="w_bf", align_bytes=64)
+        y = [keep.tile([P, T], F32, name=f"y{t}", align_bytes=64) for t in range(PACK)]
+        zeros = keep.tile([P, SPARE], F32, name="zeros", align_bytes=64)
+        nc.vector.memset(zeros[:], 0.0)
+        warm = keep.tile([P, SPARE], F32, name="warm", align_bytes=64)
+        nc.scalar.activation(warm[:], zeros[:], ACT.Gelu_apprx_tanh)
+
+        w_bf = [keep.tile([P, 2, P, PACK], BF16, name=f"w_bf{u}", align_bytes=64) for u in range(2)]
         w_codes = keep.tile([P, N], U32, name="w_codes", align_bytes=64)
         w_scale = keep.tile([P, N], U8, name="w_scale", align_bytes=64)
 
         def round_w(copy, h, t0, t1):
+            u = t0 // 2
             copy(
-                out=w_bf[:, t0:t1, :, 2 * h : 2 * h + 2].rearrange("p t m j -> p m t j"),
+                out=w_bf[u][:, t0 - 2 * u : t1 - 2 * u, :, 2 * h : 2 * h + 2].rearrange("p t m j -> p m t j"),
                 in_=w_raw[h][:].rearrange("p j (m t) -> p m t j", t=PACK)[:, :, t0:t1, :],
             )
 
         def quantize_w(t0, t1):
+            u = t0 // 2
             nc.vector.quantize_mx(
                 out=w_codes[:, t0 * P : t1 * P].bitcast(FP8X4),
                 scales=w_scale[:, t0 * P : t1 * P],
-                in_=w_bf[:, t0:t1].rearrange("p t m j -> p (t m j)"),
+                in_=w_bf[u][:, t0 - 2 * u : t1 - 2 * u].rearrange("p t m j -> p (t m j)"),
             )
-
-        y = [keep.tile([P, T], F32, name=f"y{t}", align_bytes=64) for t in range(PACK)]
 
         def project(t, c0, c1):
             acc = psum.tile([P, c1 - c0], F32, name="acc", bufs=4)
@@ -91,15 +95,16 @@ def tile_picked_wlerp_gelu_lo_kernel(
             )
             nc.scalar.activation(y[t][:, c0:c1], acc[:], ACT.Gelu_apprx_tanh)
 
-        round_w(nc.vector.tensor_copy, 0, 0, PACK)
+        round_w(nc.vector.tensor_copy, 0, 0, 2)
+        round_w(nc.scalar.copy, 0, 2, 4)
         round_w(nc.vector.tensor_copy, 1, 0, 1)
-        quantize_w(0, 1)
-        project(0, 0, T // 2)
-        project(0, T // 2, T)
         round_w(nc.vector.tensor_copy, 1, 1, 2)
+        round_w(nc.scalar.copy, 1, 2, 4)
+        quantize_w(0, 1)
+        project(0, 0, HALF)
+        project(0, HALF, T)
         quantize_w(1, 2)
         project(1, 0, T)
-        round_w(nc.vector.tensor_copy, 1, 2, PACK)
         quantize_w(2, 4)
         project(2, 0, T)
         project(3, 0, T)
@@ -109,7 +114,6 @@ def tile_picked_wlerp_gelu_lo_kernel(
         out_rows = out_0.rearrange("(p t) v -> p t v", t=PACK)
         out_words = out_1[0].rearrange("p n t -> p (n t)").bitcast(I32)
         o_scale = keep.tile([P, T], U8, name="o_scale", align_bytes=64)
-
         o_bf = keep.tile([P, T, PACK], BF16, name="o_bf", align_bytes=64)
         o_codes = keep.tile([P, T], U32, name="o_codes", align_bytes=64)
 
@@ -120,58 +124,68 @@ def tile_picked_wlerp_gelu_lo_kernel(
                 in_=o_bf[:, v0:v1, :].rearrange("p v t -> p (v t)"),
             )
 
-        def store_codes(v0, v1):
-            nc.sync.dma_start(out=out_words[:, v0:v1], in_=o_codes[:, v0:v1].bitcast(I32))
-
         def gather(dst_r, dst_l, t, v0, v1):
             cols = slice(v0 // STRIPE, v1 // STRIPE)
             nc.vector.tensor_tensor(dst_r, y[t][:].indirect(right_offs[:, cols]), f_right[:, v0:v1], ALU.mult)
             nc.vector.tensor_tensor(dst_l, y[t][:].indirect(left_offs[:, cols]), f_left[:, v0:v1], ALU.mult)
 
-        def add_on_tensor(v0):
-            turned = psum.tile([P, PACK, P], F32, name="turned", bufs=2)
-            for t in range(PACK):
-                terms = keep.tile([P, 2, P], F32, name="terms", bufs=RING, align_bytes=64)
-                gather(terms[:, 0, :], terms[:, 1, :], t, v0, v0 + P)
-                nc.tensor.matmul(turned[:, t, :], terms[:, 0, :], ident[:], start=True, stop=False, is_transpose=True)
-                nc.tensor.matmul(turned[:, t, :], terms[:, 1, :], ident[:], start=False, stop=True, is_transpose=True)
-            turned_sb = keep.tile([P, PACK, P], F32, name=f"staging{v0}", align_bytes=64)
-            nc.scalar.copy(out=turned_sb[:], in_=turned[:])
-            back = psum.tile([P, PACK, P], F32, name="back", bufs=2)
-            for t in range(PACK):
-                nc.tensor.transpose(back[:, t, :], turned_sb[:, t, :], ident[:])
-            o = keep.tile([P, PACK, P], F32, name=f"o{v0}", align_bytes=64)
-            nc.scalar.copy(out=o[:], in_=back[:])
-            nc.sync.dma_start(out=out_rows[:, :, v0 : v0 + P], in_=o[:])
-            nc.scalar.copy(out=o_bf[:, v0 : v0 + P, :], in_=back[:].rearrange("p t v -> p v t"))
+        def terms(name):
+            tile = keep.tile([P, 2, HALF], F32, name=name, align_bytes=64)
+            return tile[:, 0, :], tile[:, 1, :]
 
-        def add_on_vector(v0, v1):
-            terms = keep.tile([P, 2, PACK, v1 - v0], F32, name="terms", bufs=RING, align_bytes=64)
-            for t in range(PACK):
-                gather(terms[:, 0, t, :], terms[:, 1, t, :], t, v0, v1)
-            o = keep.tile([P, PACK, v1 - v0], F32, name=f"staging{v0 - P}", align_bytes=64)
-            nc.vector.tensor_tensor(o[:], terms[:, 0], terms[:, 1], ALU.add)
-            nc.sync.dma_start(out=out_rows[:, :, v0:v1], in_=o[:])
-            copy = nc.vector.tensor_copy if v1 == T else nc.scalar.copy
-            copy(
-                out=o_bf[:, v0:v1, :].rearrange("p (c i) t -> p c t i", i=4),
-                in_=o[:].rearrange("p t (c i) -> p c t i", i=4),
-            )
+        def gather_and_turn(u, v0, places, bank_tag, staging_tag):
+            bank = psum.tile([P, PACK, P], F32, name=bank_tag)
+            for slot in range(2):
+                term_r, term_l = places[slot]()
+                gather(term_r, term_l, 2 * u + slot, v0, v0 + HALF)
+                for c in range(2):
+                    cols = slice(c * P, (c + 1) * P)
+                    dst = bank[:, 2 * slot + c, :]
+                    nc.tensor.matmul(dst, term_r[:, cols], ident[:], start=True, stop=False, is_transpose=True)
+                    nc.tensor.matmul(dst, term_l[:, cols], ident[:], start=False, stop=True, is_transpose=True)
+            staging = keep.tile([P, PACK, P], F32, name=staging_tag, align_bytes=64)
+            nc.scalar.copy(out=staging[:], in_=bank[:])
+            return staging
 
-        v0 = 0
-        for c, width in enumerate(CHUNKS):
-            v1 = v0 + width
-            if v1 <= ON_TENSOR:
-                add_on_tensor(v0)
-            else:
-                add_on_vector(v0, v1)
-            if v1 == T // 2:
-                quantize_out(0, v1)
-                store_codes(0, v1)
-            elif v1 > T // 2:
-                quantize_out(v0, v1)
-            v0 = v1
-        store_codes(T // 2, T)
+        def turn_back(staging, bank_tag, u, v0):
+            back = psum.tile([P, PACK, P], F32, name=bank_tag)
+            for c in range(PACK):
+                nc.tensor.transpose(back[:, c, :], staging[:, c, :], ident[:])
+            sums = back[:].rearrange("p (t c) v -> p t (c v)", t=2)
+            nc.scalar.copy(out=o_bf[:, v0 : v0 + HALF, 2 * u : 2 * u + 2], in_=sums.rearrange("p t v -> p v t"))
+            return sums
+
+        def store_sums(sums, u, v0):
+            o = keep.tile([P, 2, HALF], F32, name=f"o{u}{v0}", align_bytes=64)
+            nc.scalar.copy(out=o[:], in_=sums)
+            nc.sync.dma_start(out=out_rows[:, 2 * u : 2 * u + 2, v0 : v0 + HALF], in_=o[:])
+
+        staged1 = gather_and_turn(0, 0, [lambda: terms("terms0"), lambda: terms("terms1")], "bank_a", "staging1")
+        store_sums(turn_back(staged1, "bank_c", 0, 0), 0, 0)
+        staged2 = gather_and_turn(1, 0, [lambda: terms("terms2"), lambda: terms("terms3")], "bank_a", "staging2")
+        staged3 = gather_and_turn(
+            0, HALF, [lambda: (f_right[:, :HALF], f_left[:, :HALF]), lambda: terms("terms2")], "bank_c", "staging3"
+        )
+        sums2 = turn_back(staged2, "bank_b", 1, 0)
+        sums3 = turn_back(staged3, "bank_a", 0, HALF)
+        store_sums(sums2, 1, 0)
+        store_sums(sums3, 0, HALF)
+
+        o = keep.tile([P, 2, HALF], F32, name="staging2", align_bytes=64)
+        last = [terms("terms3"), terms("y1")]
+        for slot in range(2):
+            gather(last[slot][0], last[slot][1], 2 + slot, HALF, T)
+        for slot in range(2):
+            nc.vector.tensor_tensor(o[:, slot, :], last[slot][0], last[slot][1], ALU.add)
+        nc.sync.dma_start(out=out_rows[:, 2:4, HALF:], in_=o[:])
+        nc.vector.tensor_copy(
+            out=o_bf[:, HALF:, 2:4].rearrange("p (c i) t -> p c t i", i=4),
+            in_=o[:].rearrange("p t (c i) -> p c t i", i=4),
+        )
+        quantize_out(0, HALF)
+        quantize_out(HALF, T)
+
+        nc.sync.dma_start(out=out_words, in_=o_codes[:].bitcast(I32))
         for q in range(4):
             queue = nc.scalar if q % 2 else nc.sync
             queue.dma_start(

@@ -31,10 +31,6 @@ def tile_picked_wlerp_gelu_lo_kernel(
         keep = ctx.enter_context(tc.tile_pool(name="keep", bufs=1))
         psum = ctx.enter_context(tc.psum_pool(name="psum", bufs=1))
 
-        right_offs = keep.tile([P, T // STRIPE], U16, name="right_offs")
-        nc.sync.dma_start(right_offs[:], right)
-        left_offs = keep.tile([P, T // STRIPE], U16, name="left_offs")
-        nc.sync.dma_start(left_offs[:], left)
         w_rows = w1.rearrange("(p j) m -> p j m", j=PACK)
         w_raw = [keep.tile([P, 2, N], F32, name=f"w_raw{h}", align_bytes=64) for h in range(2)]
         for h in range(2):
@@ -46,12 +42,15 @@ def tile_picked_wlerp_gelu_lo_kernel(
             in_=x_words[0].rearrange("p n t -> p (n t)").bitcast(I32),
         )
         x_scale = keep.tile([P, T], U8, name="x_scale", align_bytes=64)
-        nc.vector.memset(x_scale[:].bitcast(U32), 0)
         for q in range(4):
             nc.scalar.dma_start(
                 out=x_scale[32 * q : 32 * q + 4, :].bitcast(I32),
                 in_=x_scales[0, 4 * q : 4 * q + 4, :].bitcast(I32),
             )
+        right_offs = keep.tile([P, T // STRIPE], U16, name="right_offs")
+        nc.sync.dma_start(right_offs[:], right)
+        left_offs = keep.tile([P, T // STRIPE], U16, name="left_offs")
+        nc.sync.dma_start(left_offs[:], left)
         f_right = keep.tile([P, T], F32, name="f_right", align_bytes=64)
         nc.sync.dma_start(out=f_right[:], in_=frac)
         ident = keep.tile([P, P], F32, name="ident", align_bytes=64)
@@ -83,7 +82,7 @@ def tile_picked_wlerp_gelu_lo_kernel(
             )
 
         def project(t, c0, c1):
-            acc = psum.tile([P, c1 - c0], F32, name="acc", bufs=4)
+            acc = psum.tile([P, c1 - c0], F32, name="acc", bufs=3)
             nc.tensor.matmul_mx(
                 out=acc[:],
                 lhsT=w_codes[:, t * P : (t + 1) * P].bitcast(FP8X4),
@@ -133,45 +132,41 @@ def tile_picked_wlerp_gelu_lo_kernel(
             tile = keep.tile([P, 2, HALF], F32, name=name, align_bytes=64)
             return tile[:, 0, :], tile[:, 1, :]
 
-        def gather_and_turn(u, v0, places, bank_tag, staging_tag):
-            bank = psum.tile([P, PACK, P], F32, name=bank_tag)
-            for slot in range(2):
-                term_r, term_l = places[slot]()
-                gather(term_r, term_l, 2 * u + slot, v0, v0 + HALF)
-                for c in range(2):
-                    cols = slice(c * P, (c + 1) * P)
-                    dst = bank[:, 2 * slot + c, :]
-                    nc.tensor.matmul(dst, term_r[:, cols], ident[:], start=True, stop=False, is_transpose=True)
-                    nc.tensor.matmul(dst, term_l[:, cols], ident[:], start=False, stop=True, is_transpose=True)
-            staging = keep.tile([P, PACK, P], F32, name=staging_tag, align_bytes=64)
-            nc.scalar.copy(out=staging[:], in_=bank[:])
-            return staging
+        def add_on_tensor(back, t, v0, term_r, term_l):
+            gather(term_r, term_l, t, v0, v0 + HALF)
+            turned = psum.tile([P, 2, P], F32, name="turned", bufs=2)
+            for c in range(2):
+                cols = slice(c * P, (c + 1) * P)
+                nc.tensor.matmul(turned[:, c, :], term_r[:, cols], ident[:], start=True, stop=False, is_transpose=True)
+                nc.tensor.matmul(turned[:, c, :], term_l[:, cols], ident[:], start=False, stop=True, is_transpose=True)
+            staging = keep.tile([P, 2, P], F32, name=f"staging{t}{v0}", align_bytes=64)
+            nc.scalar.copy(out=staging[:], in_=turned[:])
+            for c in range(2):
+                nc.tensor.transpose(back[:, t % 2, c * P : (c + 1) * P], staging[:, c, :], ident[:])
 
-        def turn_back(staging, bank_tag, u, v0):
-            back = psum.tile([P, PACK, P], F32, name=bank_tag)
-            for c in range(PACK):
-                nc.tensor.transpose(back[:, c, :], staging[:, c, :], ident[:])
-            sums = back[:].rearrange("p (t c) v -> p t (c v)", t=2)
-            nc.scalar.copy(out=o_bf[:, v0 : v0 + HALF, 2 * u : 2 * u + 2], in_=sums.rearrange("p t v -> p v t"))
-            return sums
+        def round_sums(back, u, v0):
+            nc.scalar.copy(out=o_bf[:, v0 : v0 + HALF, 2 * u : 2 * u + 2], in_=back[:].rearrange("p t v -> p v t"))
 
-        def store_sums(sums, u, v0):
+        def store_sums(back, u, v0):
             o = keep.tile([P, 2, HALF], F32, name=f"o{u}{v0}", align_bytes=64)
-            nc.scalar.copy(out=o[:], in_=sums)
+            nc.scalar.copy(out=o[:], in_=back[:])
             nc.sync.dma_start(out=out_rows[:, 2 * u : 2 * u + 2, v0 : v0 + HALF], in_=o[:])
 
-        staged1 = gather_and_turn(0, 0, [lambda: terms("terms0"), lambda: terms("terms1")], "bank_a", "staging1")
-        store_sums(turn_back(staged1, "bank_c", 0, 0), 0, 0)
-        staged2 = gather_and_turn(1, 0, [lambda: terms("terms2"), lambda: terms("terms3")], "bank_a", "staging2")
-        staged3 = gather_and_turn(
-            0, HALF, [lambda: (f_right[:, :HALF], f_left[:, :HALF]), lambda: terms("terms2")], "bank_c", "staging3"
-        )
-        sums2 = turn_back(staged2, "bank_b", 1, 0)
-        sums3 = turn_back(staged3, "bank_a", 0, HALF)
-        store_sums(sums2, 1, 0)
-        store_sums(sums3, 0, HALF)
+        backs = [psum.tile([P, 2, HALF], F32, name=f"back{i}") for i in range(3)]
+        add_on_tensor(backs[0], 0, 0, *terms("terms0"))
+        add_on_tensor(backs[0], 1, 0, *terms("terms1"))
+        round_sums(backs[0], 0, 0)
+        add_on_tensor(backs[1], 2, 0, *terms("terms2"))
+        add_on_tensor(backs[1], 3, 0, *terms("terms3"))
+        store_sums(backs[0], 0, 0)
+        add_on_tensor(backs[2], 0, HALF, f_right[:, :HALF], f_left[:, :HALF])
+        round_sums(backs[1], 1, 0)
+        add_on_tensor(backs[2], 1, HALF, *terms("terms2"))
+        store_sums(backs[1], 1, 0)
+        round_sums(backs[2], 0, HALF)
+        store_sums(backs[2], 0, HALF)
 
-        o = keep.tile([P, 2, HALF], F32, name="staging2", align_bytes=64)
+        o = keep.tile([P, 2, HALF], F32, name=f"staging0{HALF}", align_bytes=64)
         last = [terms("terms3"), terms("y1")]
         for slot in range(2):
             gather(last[slot][0], last[slot][1], 2 + slot, HALF, T)
@@ -182,10 +177,10 @@ def tile_picked_wlerp_gelu_lo_kernel(
             out=o_bf[:, HALF:, 2:4].rearrange("p (c i) t -> p c t i", i=4),
             in_=o[:].rearrange("p t (c i) -> p c t i", i=4),
         )
-        quantize_out(0, HALF)
-        quantize_out(HALF, T)
+        for v0 in (0, HALF):
+            quantize_out(v0, v0 + HALF)
+            nc.sync.dma_start(out=out_words[:, v0 : v0 + HALF], in_=o_codes[:, v0 : v0 + HALF].bitcast(I32))
 
-        nc.sync.dma_start(out=out_words, in_=o_codes[:].bitcast(I32))
         for q in range(4):
             queue = nc.scalar if q % 2 else nc.sync
             queue.dma_start(

@@ -114,11 +114,10 @@ def tile_picked_wlerp_gelu_lo_kernel(
         out_words = out_1[0].rearrange("p n t -> p (n t)").bitcast(I32)
         o_scale = keep.tile([P, T], U8, name="o_scale", align_bytes=64)
         o_bf = keep.tile([P, T, PACK], BF16, name="o_bf", align_bytes=64)
-        o_codes = keep.tile([P, T], U32, name="o_codes", align_bytes=64)
 
-        def quantize_out(v0, v1):
+        def quantize_out(codes, v0, v1):
             nc.vector.quantize_mx(
-                out=o_codes[:, v0:v1].bitcast(FP8X4),
+                out=codes[:].bitcast(FP8X4),
                 scales=o_scale[:, v0:v1],
                 in_=o_bf[:, v0:v1, :].rearrange("p v t -> p (v t)"),
             )
@@ -177,9 +176,10 @@ def tile_picked_wlerp_gelu_lo_kernel(
             out=o_bf[:, HALF:, 2:4].rearrange("p (c i) t -> p c t i", i=4),
             in_=o[:].rearrange("p t (c i) -> p c t i", i=4),
         )
-        for v0 in (0, HALF):
-            quantize_out(v0, v0 + HALF)
-            nc.sync.dma_start(out=out_words[:, v0 : v0 + HALF], in_=o_codes[:, v0 : v0 + HALF].bitcast(I32))
+        for v0, tag in ((0, "terms3"), (HALF, "codes_late")):
+            codes = keep.tile([P, HALF], U32, name=tag, align_bytes=64)
+            quantize_out(codes, v0, v0 + HALF)
+            nc.sync.dma_start(out=out_words[:, v0 : v0 + HALF], in_=codes[:].bitcast(I32))
 
         for q in range(4):
             queue = nc.scalar if q % 2 else nc.sync

@@ -162,21 +162,24 @@ def tile_picked_wlerp_gelu_lo_kernel(
         round_sums(backs[1], 1, 0)
         add_on_tensor(backs[2], 1, HALF, *terms("terms2"))
         store_sums(backs[1], 1, 0)
-        round_sums(backs[2], 0, HALF)
         store_sums(backs[2], 0, HALF)
+        round_sums(backs[2], 0, HALF)
 
         o = keep.tile([P, 2, HALF], F32, name=f"staging0{HALF}", align_bytes=64)
         last = [terms("terms3"), terms("y1")]
         for slot in range(2):
             gather(last[slot][0], last[slot][1], 2 + slot, HALF, T)
-        for slot in range(2):
-            nc.vector.tensor_tensor(o[:, slot, :], last[slot][0], last[slot][1], ALU.add)
+        nc.vector.tensor_tensor(o[:, 0, :], last[0][0], last[0][1], ALU.add)
+        for c0 in (0, P):
+            cols = slice(c0, c0 + P)
+            nc.vector.tensor_tensor(o[:, 1, cols], last[1][0][:, cols], last[1][1][:, cols], ALU.add)
         nc.sync.dma_start(out=out_rows[:, 2:4, HALF:], in_=o[:])
-        nc.vector.tensor_copy(
-            out=o_bf[:, HALF:, 2:4].rearrange("p (c i) t -> p c t i", i=4),
-            in_=o[:].rearrange("p t (c i) -> p c t i", i=4),
-        )
-        for v0, tag in ((0, "terms3"), (HALF, "codes_late")):
+        for c0 in (0, P):
+            nc.vector.tensor_copy(
+                out=o_bf[:, HALF + c0 : HALF + c0 + P, 2:4].rearrange("p (c i) t -> p c t i", i=4),
+                in_=o[:, :, c0 : c0 + P].rearrange("p t (c i) -> p c t i", i=4),
+            )
+        for v0, tag in ((0, "y1"), (HALF, "codes_late")):
             codes = keep.tile([P, HALF], U32, name=tag, align_bytes=64)
             quantize_out(codes, v0, v0 + HALF)
             nc.sync.dma_start(out=out_words[:, v0 : v0 + HALF], in_=codes[:].bitcast(I32))

@@ -20,6 +20,7 @@ P = 128
 PACK = 4
 STRIPE = 16
 HALF = T // 2
+WORDS = P // 2
 SPARE = 16
 
 
@@ -31,144 +32,176 @@ def tile_picked_wlerp_gelu_lo_kernel(
         keep = ctx.enter_context(tc.tile_pool(name="keep", bufs=1))
         psum = ctx.enter_context(tc.psum_pool(name="psum", bufs=1))
 
-        w_rows = w1.rearrange("(p j) m -> p j m", j=PACK)
-        w_raw = [keep.tile([P, 2, N], F32, name=f"w_raw{h}", align_bytes=64) for h in range(2)]
-        for h in range(2):
-            nc.sync.dma_start(out=w_raw[h][:], in_=w_rows[:, 2 * h : 2 * h + 2, :])
+        def sbuf(name, shape, dtype):
+            return keep.tile(shape, dtype, name=name, align_bytes=64)
 
-        x_codes = keep.tile([P, T], U32, name="x_codes", align_bytes=64)
+        w_rows = w1.rearrange("(p j) m -> p j m", j=PACK)
+        w_raw = [sbuf(f"w_raw{s}", [P, PACK, N // 2], F32) for s in range(2)]
+        x_codes = sbuf("x_codes", [P, T], U32)
+        x_scale = sbuf("x_scale", [P, T], U8)
+        f_cols = sbuf("f_cols", [P, PACK], F32)
+        right_offs = keep.tile([P, T // STRIPE], U16, name="right_offs")
+        left_offs = keep.tile([P, T // STRIPE], U16, name="left_offs")
+
+        nc.scalar.dma_start(out=f_cols[:], in_=frac[0].rearrange("(p c) -> p c", c=PACK))
+        nc.sync.dma_start(out=w_raw[0][:], in_=w_rows[:, :, : N // 2])
         nc.sync.dma_start(
             out=x_codes[:].bitcast(I32),
             in_=x_words[0].rearrange("p n t -> p (n t)").bitcast(I32),
         )
-        x_scale = keep.tile([P, T], U8, name="x_scale", align_bytes=64)
         for q in range(4):
-            nc.scalar.dma_start(
+            queue = nc.scalar if q < 2 else nc.sync
+            queue.dma_start(
                 out=x_scale[32 * q : 32 * q + 4, :].bitcast(I32),
                 in_=x_scales[0, 4 * q : 4 * q + 4, :].bitcast(I32),
             )
-        right_offs = keep.tile([P, T // STRIPE], U16, name="right_offs")
+        nc.sync.dma_start(out=w_raw[1][:], in_=w_rows[:, :, N // 2 :])
         nc.sync.dma_start(right_offs[:], right)
-        left_offs = keep.tile([P, T // STRIPE], U16, name="left_offs")
         nc.sync.dma_start(left_offs[:], left)
-        f_right = keep.tile([P, T], F32, name="f_right", align_bytes=64)
-        nc.sync.dma_start(out=f_right[:], in_=frac)
-        ident = keep.tile([P, P], F32, name="ident", align_bytes=64)
-        make_identity(nc, ident[:])
 
-        y = [keep.tile([P, T], F32, name=f"y{t}", align_bytes=64) for t in range(PACK)]
-        zeros = keep.tile([P, SPARE], F32, name="zeros", align_bytes=64)
+        ident = sbuf("ident", [P, P], F32)
+        make_identity(nc, ident[:])
+        zeros = sbuf("zeros", [P, SPARE], F32)
         nc.vector.memset(zeros[:], 0.0)
-        warm = keep.tile([P, SPARE], F32, name="warm", align_bytes=64)
+        warm = sbuf("warm", [P, SPARE], F32)
         nc.scalar.activation(warm[:], zeros[:], ACT.Gelu_apprx_tanh)
 
-        w_bf = [keep.tile([P, 2, P, PACK], BF16, name=f"w_bf{u}", align_bytes=64) for u in range(2)]
-        w_codes = keep.tile([P, N], U32, name="w_codes", align_bytes=64)
-        w_scale = keep.tile([P, N], U8, name="w_scale", align_bytes=64)
+        f_bank = psum.tile([P, PACK, P], F32, name="acc", bufs=3)
+        for c in range(PACK):
+            nc.tensor.transpose(f_bank[:, c, :], f_cols[:, c : c + 1].to_broadcast([P, P]), ident[:])
+        f_right = sbuf("f_right", [P, T], F32)
+        nc.scalar.copy(out=f_right[:].rearrange("q (p c) -> q p c", c=PACK), in_=f_bank[:].rearrange("q c p -> q p c"))
 
-        def round_w(copy, h, t0, t1):
-            u = t0 // 2
+        y = [sbuf(f"y{i}", [P, T], F32) for i in range(4)]
+        w_codes = [sbuf(f"w_codes{i}", [P, P], U32) for i in range(4)]
+        w_scale = [sbuf(f"w_scale{i}", [P, P], U8) for i in range(4)]
+        w_bf = [[sbuf(f"w_bf0{u}", [P, 2, WORDS, PACK], BF16) for u in range(2)]]
+
+        def round_w(copy, s, u, l0, l1):
             copy(
-                out=w_bf[u][:, t0 - 2 * u : t1 - 2 * u, :, 2 * h : 2 * h + 2].rearrange("p t m j -> p m t j"),
-                in_=w_raw[h][:].rearrange("p j (m t) -> p m t j", t=PACK)[:, :, t0:t1, :],
+                out=w_bf[s][u][:, :, l0:l1, :].rearrange("p t l j -> p l t j"),
+                in_=w_raw[s][:].rearrange("p j (l t) -> p l t j", t=PACK)[:, l0:l1, 2 * u : 2 * u + 2, :],
             )
 
-        def quantize_w(t0, t1):
-            u = t0 // 2
-            nc.vector.quantize_mx(
-                out=w_codes[:, t0 * P : t1 * P].bitcast(FP8X4),
-                scales=w_scale[:, t0 * P : t1 * P],
-                in_=w_bf[u][:, t0 - 2 * u : t1 - 2 * u].rearrange("p t m j -> p (t m j)"),
-            )
+        def quantize_w(i, c0, src):
+            c1 = c0 + src.shape[1] // PACK
+            nc.vector.quantize_mx(out=w_codes[i][:, c0:c1].bitcast(FP8X4), scales=w_scale[i][:, c0:c1], in_=src)
 
-        def project(t, c0, c1):
+        def quantize_folded(s):
+            quantize_w(s, 0, w_bf[s][0][:].rearrange("p t l j -> p (t l j)"))
+
+        def quantize_plain(s):
+            for t in range(2):
+                quantize_w(2 + t, s * WORDS, w_bf[s][1][:, t].rearrange("p l j -> p (l j)"))
+
+        def project(i, c0, c1):
             acc = psum.tile([P, c1 - c0], F32, name="acc", bufs=3)
             nc.tensor.matmul_mx(
                 out=acc[:],
-                lhsT=w_codes[:, t * P : (t + 1) * P].bitcast(FP8X4),
-                lhsT_scale=w_scale[:, t * P : (t + 1) * P],
+                lhsT=w_codes[i][:].bitcast(FP8X4),
+                lhsT_scale=w_scale[i][:],
                 rhs=x_codes[:, c0:c1].bitcast(FP8X4),
                 rhs_scale=x_scale[:, c0:c1],
                 start=True,
                 stop=True,
             )
-            nc.scalar.activation(y[t][:, c0:c1], acc[:], ACT.Gelu_apprx_tanh)
+            nc.scalar.activation(y[i][:, c0:c1], acc[:], ACT.Gelu_apprx_tanh)
 
-        round_w(nc.vector.tensor_copy, 0, 0, 2)
-        round_w(nc.scalar.copy, 0, 2, 4)
-        round_w(nc.vector.tensor_copy, 1, 0, 1)
-        round_w(nc.vector.tensor_copy, 1, 1, 2)
-        round_w(nc.scalar.copy, 1, 2, 4)
-        quantize_w(0, 1)
-        project(0, 0, HALF)
-        project(0, HALF, T)
-        quantize_w(1, 2)
-        project(1, 0, T)
-        quantize_w(2, 4)
-        project(2, 0, T)
-        project(3, 0, T)
-        f_left = keep.tile([P, T], F32, name="f_left", align_bytes=64)
-        nc.vector.tensor_scalar(f_left[:], f_right[:], -1.0, 1.0, ALU.mult, ALU.add)
+        f_left = sbuf("f_left", [P, T], F32)
+
+        def gather(dst, offs, weight, i, v0):
+            cols = slice(v0 // STRIPE, (v0 + HALF) // STRIPE)
+            nc.vector.tensor_tensor(dst, y[i][:].indirect(offs[:, cols]), weight[:, v0 : v0 + HALF], ALU.mult)
+
+        def turn(term_r, term_l, dst):
+            turned = psum.tile([P, 2, P], F32, name="turned", bufs=2)
+            for i, term in enumerate((term_r, term_l)):
+                for c in range(2):
+                    nc.tensor.matmul(
+                        turned[:, c, :],
+                        term[:, c * P : (c + 1) * P],
+                        ident[:],
+                        start=(i, c) == (0, 0),
+                        stop=(i, c) == (1, 1),
+                        is_transpose=True,
+                    )
+            nc.scalar.copy(out=dst, in_=turned[:].rearrange("v c (t l) -> v c t l", l=dst.shape[3]))
+
+        def piece(i, v0, term_r, term_l, dst):
+            gather(term_r, right_offs, f_right, i, v0)
+            gather(term_l, left_offs, f_left, i, v0)
+            turn(term_r, term_l, dst)
+
+        def terms(name):
+            tile = sbuf(name, [P, 2, HALF], F32)
+            return tile[:, 0, :], tile[:, 1, :]
+
+        def turn_back(back, staging, t):
+            for c in range(2):
+                nc.tensor.transpose(back[:, t, c * P : (c + 1) * P], staging[:, c, t, :], ident[:])
 
         out_rows = out_0.rearrange("(p t) v -> p t v", t=PACK)
         out_words = out_1[0].rearrange("p n t -> p (n t)").bitcast(I32)
-        o_scale = keep.tile([P, T], U8, name="o_scale", align_bytes=64)
-        o_bf = keep.tile([P, T, PACK], BF16, name="o_bf", align_bytes=64)
-
-        def quantize_out(codes, v0, v1):
-            nc.vector.quantize_mx(
-                out=codes[:].bitcast(FP8X4),
-                scales=o_scale[:, v0:v1],
-                in_=o_bf[:, v0:v1, :].rearrange("p v t -> p (v t)"),
-            )
-
-        def gather(dst_r, dst_l, t, v0, v1):
-            cols = slice(v0 // STRIPE, v1 // STRIPE)
-            nc.vector.tensor_tensor(dst_r, y[t][:].indirect(right_offs[:, cols]), f_right[:, v0:v1], ALU.mult)
-            nc.vector.tensor_tensor(dst_l, y[t][:].indirect(left_offs[:, cols]), f_left[:, v0:v1], ALU.mult)
-
-        def terms(name):
-            tile = keep.tile([P, 2, HALF], F32, name=name, align_bytes=64)
-            return tile[:, 0, :], tile[:, 1, :]
-
-        def add_on_tensor(back, t, v0, term_r, term_l):
-            gather(term_r, term_l, t, v0, v0 + HALF)
-            turned = psum.tile([P, 2, P], F32, name="turned", bufs=2)
-            for c in range(2):
-                cols = slice(c * P, (c + 1) * P)
-                nc.tensor.matmul(turned[:, c, :], term_r[:, cols], ident[:], start=True, stop=False, is_transpose=True)
-                nc.tensor.matmul(turned[:, c, :], term_l[:, cols], ident[:], start=False, stop=True, is_transpose=True)
-            staging = keep.tile([P, 2, P], F32, name=f"staging{t}{v0}", align_bytes=64)
-            nc.scalar.copy(out=staging[:], in_=turned[:])
-            for c in range(2):
-                nc.tensor.transpose(back[:, t % 2, c * P : (c + 1) * P], staging[:, c, :], ident[:])
+        o_scale = sbuf("o_scale", [P, T], U8)
+        o_bf = sbuf("o_bf", [P, T, PACK], BF16)
 
         def round_sums(back, u, v0):
             nc.scalar.copy(out=o_bf[:, v0 : v0 + HALF, 2 * u : 2 * u + 2], in_=back[:].rearrange("p t v -> p v t"))
 
         def store_sums(back, u, v0):
-            o = keep.tile([P, 2, HALF], F32, name=f"o{u}{v0}", align_bytes=64)
+            o = sbuf(f"o{u}{v0}", [P, 2, HALF], F32)
             nc.scalar.copy(out=o[:], in_=back[:])
             nc.sync.dma_start(out=out_rows[:, 2 * u : 2 * u + 2, v0 : v0 + HALF], in_=o[:])
 
-        backs = [psum.tile([P, 2, HALF], F32, name=f"back{i}") for i in range(3)]
-        add_on_tensor(backs[0], 0, 0, *terms("terms0"))
-        add_on_tensor(backs[0], 1, 0, *terms("terms1"))
-        round_sums(backs[0], 0, 0)
-        add_on_tensor(backs[1], 2, 0, *terms("terms2"))
-        add_on_tensor(backs[1], 3, 0, *terms("terms3"))
-        store_sums(backs[0], 0, 0)
-        add_on_tensor(backs[2], 0, HALF, f_right[:, :HALF], f_left[:, :HALF])
-        round_sums(backs[1], 1, 0)
-        add_on_tensor(backs[2], 1, HALF, *terms("terms2"))
-        store_sums(backs[1], 1, 0)
-        store_sums(backs[2], 0, HALF)
-        round_sums(backs[2], 0, HALF)
+        round_w(nc.vector.tensor_copy, 0, 0, 0, WORDS)
+        round_w(nc.vector.tensor_copy, 0, 1, 0, WORDS // 2)
+        quantize_folded(0)
+        project(0, 0, HALF)
+        project(0, HALF, T)
+        round_w(nc.vector.tensor_copy, 0, 1, WORDS // 2, WORDS)
+        nc.vector.tensor_scalar(f_left[:], f_right[:], -1.0, 1.0, ALU.mult, ALU.add)
+        quantize_plain(0)
+        w_bf.append([sbuf(name, [P, 2, WORDS, PACK], BF16) for name in ("w_codes0", "w_scale0")])
+        round_w(nc.vector.tensor_copy, 1, 0, 0, WORDS // 2)
+        round_w(nc.scalar.copy, 1, 0, WORDS // 2, WORDS)
 
-        o = keep.tile([P, 2, HALF], F32, name=f"staging0{HALF}", align_bytes=64)
-        last = [terms("terms3"), terms("y1")]
-        for slot in range(2):
-            gather(last[slot][0], last[slot][1], 2 + slot, HALF, T)
+        staging = [sbuf(f"staging{i}", [P, 2, 2, P], F32) for i in range(3)]
+        backs = [psum.tile([P, 2, HALF], F32, name=f"back{i}") for i in range(3)]
+
+        first_r = sbuf("first_r", [P, HALF], F32)
+        gather(first_r[:], right_offs, f_right, 0, 0)
+        quantize_folded(1)
+        project(1, 0, HALF)
+        project(1, HALF, T)
+        held = sbuf("w_codes0", [P, 3, HALF], F32)
+        first_l = held[:, 0, :]
+        gather(first_l, left_offs, f_left, 0, 0)
+        round_w(nc.scalar.copy, 1, 1, 0, WORDS)
+        quantize_plain(1)
+        project(2, 0, T)
+        project(3, 0, T)
+        turn(first_r[:], first_l, staging[0][:, :, :, :WORDS])
+        piece(0, HALF, held[:, 1, :], held[:, 2, :], staging[1][:, :, :, :WORDS])
+        for h in range(2):
+            piece(1, h * HALF, *terms(f"terms{2 + h}"), staging[h][:, :, :, WORDS:])
+            for t in range(2):
+                turn_back(backs[h], staging[h], t)
+        round_sums(backs[0], 0, 0)
+        store_sums(backs[0], 0, 0)
+        for t in range(2):
+            piece(2 + t, 0, *terms(f"terms{4 + t}"), staging[2][:, :, t : t + 1, :])
+            turn_back(backs[2], staging[2], t)
+            if t == 0:
+                round_sums(backs[1], 0, HALF)
+                store_sums(backs[1], 0, HALF)
+        round_sums(backs[2], 1, 0)
+        store_sums(backs[2], 1, 0)
+
+        o = sbuf("staging1", [P, 2, HALF], F32)
+        last = [(f_right[:, :HALF], f_left[:, :HALF]), terms("y1")]
+        for t in range(2):
+            gather(last[t][0], right_offs, f_right, 2 + t, HALF)
+            gather(last[t][1], left_offs, f_left, 2 + t, HALF)
         nc.vector.tensor_tensor(o[:, 0, :], last[0][0], last[0][1], ALU.add)
         for c0 in (0, P):
             cols = slice(c0, c0 + P)
@@ -179,9 +212,13 @@ def tile_picked_wlerp_gelu_lo_kernel(
                 out=o_bf[:, HALF + c0 : HALF + c0 + P, 2:4].rearrange("p (c i) t -> p c t i", i=4),
                 in_=o[:, :, c0 : c0 + P].rearrange("p t (c i) -> p c t i", i=4),
             )
-        for v0, tag in ((0, "y1"), (HALF, "codes_late")):
-            codes = keep.tile([P, HALF], U32, name=tag, align_bytes=64)
-            quantize_out(codes, v0, v0 + HALF)
+        for v0 in (0, HALF):
+            codes = sbuf(f"codes{v0}", [P, HALF], U32)
+            nc.vector.quantize_mx(
+                out=codes[:].bitcast(FP8X4),
+                scales=o_scale[:, v0 : v0 + HALF],
+                in_=o_bf[:, v0 : v0 + HALF, :].rearrange("p v t -> p (v t)"),
+            )
             nc.sync.dma_start(out=out_words[:, v0 : v0 + HALF], in_=codes[:].bitcast(I32))
 
         for q in range(4):

@@ -148,8 +148,8 @@ def tile_picked_wlerp_gelu_lo_kernel(
         def round_sums(back, u, v0):
             nc.scalar.copy(out=o_bf[:, v0 : v0 + HALF, 2 * u : 2 * u + 2], in_=back[:].rearrange("p t v -> p v t"))
 
-        def store_sums(back, u, v0):
-            o = sbuf(f"o{u}{v0}", [P, 2, HALF], F32)
+        def store_sums(back, u, v0, slot):
+            o = sbuf(slot, [P, 2, HALF], F32)
             nc.scalar.copy(out=o[:], in_=back[:])
             nc.sync.dma_start(out=out_rows[:, 2 * u : 2 * u + 2, v0 : v0 + HALF], in_=o[:])
 
@@ -184,42 +184,53 @@ def tile_picked_wlerp_gelu_lo_kernel(
         piece(0, HALF, held[:, 1, :], held[:, 2, :], staging[1][:, :, :, :WORDS])
         for h in range(2):
             piece(1, h * HALF, *terms(f"terms{2 + h}"), staging[h][:, :, :, WORDS:])
-            for t in range(2):
-                turn_back(backs[h], staging[h], t)
-        round_sums(backs[0], 0, 0)
-        store_sums(backs[0], 0, 0)
         for t in range(2):
-            piece(2 + t, 0, *terms(f"terms{4 + t}"), staging[2][:, :, t : t + 1, :])
+            turn_back(backs[0], staging[0], t)
+        round_sums(backs[0], 0, 0)
+        piece(2, 0, *terms("terms4"), staging[2][:, :, 0:1, :])
+        store_sums(backs[0], 0, 0, "terms3")
+        piece(3, 0, *terms("terms5"), staging[2][:, :, 1:2, :])
+        for t in range(2):
             turn_back(backs[2], staging[2], t)
-            if t == 0:
-                round_sums(backs[1], 0, HALF)
-                store_sums(backs[1], 0, HALF)
+        for t in range(2):
+            turn_back(backs[1], staging[1], t)
         round_sums(backs[2], 1, 0)
-        store_sums(backs[2], 1, 0)
+        store_sums(backs[2], 1, 0, "sums1")
+        o = sbuf("staging1", [P, PACK, HALF], F32)
+        nc.scalar.copy(out=o[:, 0:2, :], in_=backs[1][:])
+        nc.sync.dma_start(out=out_rows[:, 0:2, HALF:], in_=o[:, 0:2, :])
 
-        o = sbuf("staging1", [P, 2, HALF], F32)
-        last = [(f_right[:, :HALF], f_left[:, :HALF]), terms("y1")]
+        def round_whole(copy, c0):
+            copy(
+                out=o_bf[:, HALF + c0 : HALF + c0 + P, :].rearrange("p (c i) t -> p c t i", i=4),
+                in_=o[:, :, c0 : c0 + P].rearrange("p t (c i) -> p c t i", i=4),
+            )
+
+        def quantize_out(codes, v0, v1):
+            nc.vector.quantize_mx(
+                out=codes.bitcast(FP8X4),
+                scales=o_scale[:, v0:v1],
+                in_=o_bf[:, v0:v1, :].rearrange("p v t -> p (v t)"),
+            )
+
+        last = [(f_right[:, :HALF], f_left[:, :HALF]), terms("terms4")]
         for t in range(2):
             gather(last[t][0], right_offs, f_right, 2 + t, HALF)
             gather(last[t][1], left_offs, f_left, 2 + t, HALF)
-        nc.vector.tensor_tensor(o[:, 0, :], last[0][0], last[0][1], ALU.add)
+        nc.vector.tensor_tensor(o[:, 2, :], last[0][0], last[0][1], ALU.add)
         for c0 in (0, P):
             cols = slice(c0, c0 + P)
-            nc.vector.tensor_tensor(o[:, 1, cols], last[1][0][:, cols], last[1][1][:, cols], ALU.add)
-        nc.sync.dma_start(out=out_rows[:, 2:4, HALF:], in_=o[:])
+            nc.vector.tensor_tensor(o[:, 3, cols], last[1][0][:, cols], last[1][1][:, cols], ALU.add)
+        nc.sync.dma_start(out=out_rows[:, 2:4, HALF:], in_=o[:, 2:4, :])
+        round_whole(nc.scalar.copy, 0)
+        codes = sbuf("f_right", [P, HALF], U32)
+        quantize_out(codes[:], 0, HALF)
+        nc.sync.dma_start(out=out_words[:, :HALF], in_=codes[:].bitcast(I32))
+        round_whole(nc.vector.tensor_copy, P)
+        codes = sbuf("codes", [P, HALF], U32)
         for c0 in (0, P):
-            nc.vector.tensor_copy(
-                out=o_bf[:, HALF + c0 : HALF + c0 + P, 2:4].rearrange("p (c i) t -> p c t i", i=4),
-                in_=o[:, :, c0 : c0 + P].rearrange("p t (c i) -> p c t i", i=4),
-            )
-        for v0 in (0, HALF):
-            codes = sbuf(f"codes{v0}", [P, HALF], U32)
-            nc.vector.quantize_mx(
-                out=codes[:].bitcast(FP8X4),
-                scales=o_scale[:, v0 : v0 + HALF],
-                in_=o_bf[:, v0 : v0 + HALF, :].rearrange("p v t -> p (v t)"),
-            )
-            nc.sync.dma_start(out=out_words[:, v0 : v0 + HALF], in_=codes[:].bitcast(I32))
+            quantize_out(codes[:, c0 : c0 + P], HALF + c0, HALF + c0 + P)
+        nc.sync.dma_start(out=out_words[:, HALF:], in_=codes[:].bitcast(I32))
 
         for q in range(4):
             queue = nc.scalar if q % 2 else nc.sync

@@ -39,24 +39,26 @@ def tile_picked_wlerp_gelu_lo_kernel(
         w_raw = [sbuf(f"w_raw{s}", [P, PACK, N // 2], F32) for s in range(2)]
         x_codes = sbuf("x_codes", [P, T], U32)
         x_scale = sbuf("x_scale", [P, T], U8)
-        f_cols = sbuf("f_cols", [P, PACK], F32)
+        f_right = sbuf("f_right", [P, T], F32)
         right_offs = keep.tile([P, T // STRIPE], U16, name="right_offs")
         left_offs = keep.tile([P, T // STRIPE], U16, name="left_offs")
 
-        nc.scalar.dma_start(out=f_cols[:], in_=frac[0].rearrange("(p c) -> p c", c=PACK))
+        def load_scales(queue, q):
+            queue.dma_start(
+                out=x_scale[32 * q : 32 * q + 4, :].bitcast(I32),
+                in_=x_scales[0, 4 * q : 4 * q + 4, :].bitcast(I32),
+            )
+
         nc.sync.dma_start(out=w_raw[0][:], in_=w_rows[:, :, : N // 2])
         nc.sync.dma_start(
             out=x_codes[:].bitcast(I32),
             in_=x_words[0].rearrange("p n t -> p (n t)").bitcast(I32),
         )
         for q in range(4):
-            queue = nc.scalar if q < 2 else nc.sync
-            queue.dma_start(
-                out=x_scale[32 * q : 32 * q + 4, :].bitcast(I32),
-                in_=x_scales[0, 4 * q : 4 * q + 4, :].bitcast(I32),
-            )
-        nc.sync.dma_start(out=w_raw[1][:], in_=w_rows[:, :, N // 2 :])
+            load_scales(nc.scalar if q < 3 else nc.sync, q)
         nc.sync.dma_start(right_offs[:], right)
+        nc.sync.dma_start(out=w_raw[1][:], in_=w_rows[:, :, N // 2 :])
+        nc.sync.dma_start(out=f_right[:], in_=frac)
         nc.sync.dma_start(left_offs[:], left)
 
         ident = sbuf("ident", [P, P], F32)
@@ -65,12 +67,6 @@ def tile_picked_wlerp_gelu_lo_kernel(
         nc.vector.memset(zeros[:], 0.0)
         warm = sbuf("warm", [P, SPARE], F32)
         nc.scalar.activation(warm[:], zeros[:], ACT.Gelu_apprx_tanh)
-
-        f_bank = psum.tile([P, PACK, P], F32, name="acc", bufs=3)
-        for c in range(PACK):
-            nc.tensor.transpose(f_bank[:, c, :], f_cols[:, c : c + 1].to_broadcast([P, P]), ident[:])
-        f_right = sbuf("f_right", [P, T], F32)
-        nc.scalar.copy(out=f_right[:].rearrange("q (p c) -> q p c", c=PACK), in_=f_bank[:].rearrange("q c p -> q p c"))
 
         y = [sbuf(f"y{i}", [P, T], F32) for i in range(4)]
         w_codes = [sbuf(f"w_codes{i}", [P, P], U32) for i in range(4)]
@@ -107,7 +103,6 @@ def tile_picked_wlerp_gelu_lo_kernel(
             )
             nc.scalar.activation(y[i][:, c0:c1], acc[:], ACT.Gelu_apprx_tanh)
 
-        f_left = sbuf("f_left", [P, T], F32)
 
         def gather(dst, offs, weight, i, v0):
             cols = slice(v0 // STRIPE, (v0 + HALF) // STRIPE)
@@ -159,29 +154,28 @@ def tile_picked_wlerp_gelu_lo_kernel(
         project(0, 0, HALF)
         project(0, HALF, T)
         round_w(nc.vector.tensor_copy, 0, 1, WORDS // 2, WORDS)
-        nc.vector.tensor_scalar(f_left[:], f_right[:], -1.0, 1.0, ALU.mult, ALU.add)
+        w_bf.append([sbuf(name, [P, 2, WORDS, PACK], BF16) for name in ("w_bf10", "w_scale0")])
         quantize_plain(0)
-        w_bf.append([sbuf(name, [P, 2, WORDS, PACK], BF16) for name in ("w_codes0", "w_scale0")])
-        round_w(nc.vector.tensor_copy, 1, 0, 0, WORDS // 2)
-        round_w(nc.scalar.copy, 1, 0, WORDS // 2, WORDS)
+        round_w(nc.vector.tensor_copy, 1, 0, 0, WORDS)
+        quantize_folded(1)
+        project(1, 0, HALF)
+        project(1, HALF, T)
+        round_w(nc.scalar.copy, 1, 1, 0, WORDS)
+        f_left = sbuf("w_codes0", [P, T], F32)
+        nc.scalar.activation(f_left[:], f_right[:], ACT.Copy, scale=-1.0, bias=1.0)
+        first = [terms(f"terms{h}") for h in range(2)]
+        for h in range(2):
+            gather(first[h][0], right_offs, f_right, 0, h * HALF)
+        quantize_plain(1)
+        project(2, 0, T)
+        project(3, 0, T)
 
         staging = [sbuf(f"staging{i}", [P, 2, 2, P], F32) for i in range(3)]
         backs = [psum.tile([P, 2, HALF], F32, name=f"back{i}") for i in range(3)]
 
-        first_r = sbuf("first_r", [P, HALF], F32)
-        gather(first_r[:], right_offs, f_right, 0, 0)
-        quantize_folded(1)
-        project(1, 0, HALF)
-        project(1, HALF, T)
-        held = sbuf("w_codes0", [P, 3, HALF], F32)
-        first_l = held[:, 0, :]
-        gather(first_l, left_offs, f_left, 0, 0)
-        round_w(nc.scalar.copy, 1, 1, 0, WORDS)
-        quantize_plain(1)
-        project(2, 0, T)
-        project(3, 0, T)
-        turn(first_r[:], first_l, staging[0][:, :, :, :WORDS])
-        piece(0, HALF, held[:, 1, :], held[:, 2, :], staging[1][:, :, :, :WORDS])
+        for h in range(2):
+            gather(first[h][1], left_offs, f_left, 0, h * HALF)
+            turn(*first[h], staging[h][:, :, :, :WORDS])
         for h in range(2):
             piece(1, h * HALF, *terms(f"terms{2 + h}"), staging[h][:, :, :, WORDS:])
         for t in range(2):

@@ -188,8 +188,8 @@ def tile_picked_wlerp_gelu_lo_kernel(
             turn_back(backs[2], staging[2], t)
         for t in range(2):
             turn_back(backs[1], staging[1], t)
-        round_sums(backs[2], 1, 0)
         store_sums(backs[2], 1, 0, "sums1")
+        round_sums(backs[2], 1, 0)
         o = sbuf("staging1", [P, PACK, HALF], F32)
         nc.scalar.copy(out=o[:, 0:2, :], in_=backs[1][:])
         nc.sync.dma_start(out=out_rows[:, 0:2, HALF:], in_=o[:, 0:2, :])

@@ -160,21 +160,22 @@ def tile_picked_wlerp_gelu_lo_kernel(
         quantize_folded(1)
         project(1, 0, HALF)
         project(1, HALF, T)
-        round_w(nc.scalar.copy, 1, 1, 0, WORDS)
         f_left = sbuf("w_codes0", [P, T], F32)
         nc.scalar.activation(f_left[:], f_right[:], ACT.Copy, scale=-1.0, bias=1.0)
+        round_w(nc.scalar.copy, 1, 1, 0, WORDS)
         first = [terms(f"terms{h}") for h in range(2)]
         for h in range(2):
             gather(first[h][0], right_offs, f_right, 0, h * HALF)
+        gather(first[0][1], left_offs, f_left, 0, 0)
         quantize_plain(1)
         project(2, 0, T)
         project(3, 0, T)
+        gather(first[1][1], left_offs, f_left, 0, HALF)
 
         staging = [sbuf(f"staging{i}", [P, 2, 2, P], F32) for i in range(3)]
         backs = [psum.tile([P, 2, HALF], F32, name=f"back{i}") for i in range(3)]
 
         for h in range(2):
-            gather(first[h][1], left_offs, f_left, 0, h * HALF)
             turn(*first[h], staging[h][:, :, :, :WORDS])
         for h in range(2):
             piece(1, h * HALF, *terms(f"terms{2 + h}"), staging[h][:, :, :, WORDS:])
@@ -216,11 +217,11 @@ def tile_picked_wlerp_gelu_lo_kernel(
             cols = slice(c0, c0 + P)
             nc.vector.tensor_tensor(o[:, 3, cols], last[1][0][:, cols], last[1][1][:, cols], ALU.add)
         nc.sync.dma_start(out=out_rows[:, 2:4, HALF:], in_=o[:, 2:4, :])
-        round_whole(nc.scalar.copy, 0)
+        round_whole(nc.scalar.copy, P)
         codes = sbuf("f_right", [P, HALF], U32)
         quantize_out(codes[:], 0, HALF)
         nc.sync.dma_start(out=out_words[:, :HALF], in_=codes[:].bitcast(I32))
-        round_whole(nc.vector.tensor_copy, P)
+        round_whole(nc.vector.tensor_copy, 0)
         codes = sbuf("codes", [P, HALF], U32)
         for c0 in (0, P):
             quantize_out(codes[:, c0 : c0 + P], HALF + c0, HALF + c0 + P)

@@ -50,14 +50,14 @@ def tile_picked_wlerp_gelu_lo_kernel(
             )
 
         nc.sync.dma_start(out=w_raw[0][:], in_=w_rows[:, :, : N // 2])
+        for q in range(4):
+            load_scales(nc.scalar if q < 3 else nc.sync, q)
+        nc.sync.dma_start(out=w_raw[1][:], in_=w_rows[:, :, N // 2 :])
         nc.sync.dma_start(
             out=x_codes[:].bitcast(I32),
             in_=x_words[0].rearrange("p n t -> p (n t)").bitcast(I32),
         )
-        for q in range(4):
-            load_scales(nc.scalar if q < 3 else nc.sync, q)
         nc.sync.dma_start(right_offs[:], right)
-        nc.sync.dma_start(out=w_raw[1][:], in_=w_rows[:, :, N // 2 :])
         nc.sync.dma_start(out=f_right[:], in_=frac)
         nc.sync.dma_start(left_offs[:], left)
 
@@ -68,30 +68,32 @@ def tile_picked_wlerp_gelu_lo_kernel(
         warm = sbuf("warm", [P, SPARE], F32)
         nc.scalar.activation(warm[:], zeros[:], ACT.Gelu_apprx_tanh)
 
-        y = [sbuf(f"y{i}", [P, T], F32) for i in range(4)]
-        w_codes = [sbuf(f"w_codes{i}", [P, P], U32) for i in range(4)]
-        w_scale = [sbuf(f"w_scale{i}", [P, P], U8) for i in range(4)]
-        w_bf = [[sbuf(f"w_bf0{u}", [P, 2, WORDS, PACK], BF16) for u in range(2)]]
+        y = [sbuf(f"y{i}", [P, T + SPARE if i < 3 else T], F32) for i in range(4)]
+        for i in range(3):
+            nc.gpsimd.memset(y[i][:, T:], 0.0)
+        w_codes = [sbuf(f"w_codes{t}", [P, P], U32) for t in range(PACK)]
+        w_scale = [sbuf(f"w_scale{t}", [P, P], U8) for t in range(PACK)]
+        def round_w(name, s, t0, t1):
+            dst = sbuf(name, [P, t1 - t0, WORDS, PACK], BF16)
+            nc.vector.tensor_copy(
+                out=dst[:].rearrange("p t l j -> p l t j"),
+                in_=w_raw[s][:].rearrange("p j (l t) -> p l t j", t=PACK)[:, :, t0:t1, :],
+            )
+            return dst
 
-        def round_w(copy, s, u, l0, l1):
-            copy(
-                out=w_bf[s][u][:, :, l0:l1, :].rearrange("p t l j -> p l t j"),
-                in_=w_raw[s][:].rearrange("p j (l t) -> p l t j", t=PACK)[:, l0:l1, 2 * u : 2 * u + 2, :],
+        def quantize_w(src, s, t):
+            words = slice(s * WORDS, (s + 1) * WORDS)
+            nc.vector.quantize_mx(
+                out=w_codes[t][:, words].bitcast(FP8X4),
+                scales=w_scale[t][:, words],
+                in_=src.rearrange("p l j -> p (l j)"),
             )
 
-        def quantize_w(i, c0, src):
-            c1 = c0 + src.shape[1] // PACK
-            nc.vector.quantize_mx(out=w_codes[i][:, c0:c1].bitcast(FP8X4), scales=w_scale[i][:, c0:c1], in_=src)
+        def bank(b, shape):
+            return psum.tile(shape, F32, name=f"bank{b}")
 
-        def quantize_folded(s):
-            quantize_w(s, 0, w_bf[s][0][:].rearrange("p t l j -> p (t l j)"))
-
-        def quantize_plain(s):
-            for t in range(2):
-                quantize_w(2 + t, s * WORDS, w_bf[s][1][:, t].rearrange("p l j -> p (l j)"))
-
-        def project(i, c0, c1):
-            acc = psum.tile([P, c1 - c0], F32, name="acc", bufs=3)
+        def project(i, c0, c1, b):
+            acc = bank(b, [P, c1 - c0])
             nc.tensor.matmul_mx(
                 out=acc[:],
                 lhsT=w_codes[i][:].bitcast(FP8X4),
@@ -103,102 +105,44 @@ def tile_picked_wlerp_gelu_lo_kernel(
             )
             nc.scalar.activation(y[i][:, c0:c1], acc[:], ACT.Gelu_apprx_tanh)
 
+        def window(i, offs, h):
+            return y[i][:].indirect(offs[:, h * HALF // STRIPE : (h + 1) * HALF // STRIPE])
 
-        def gather(dst, offs, weight, i, v0):
-            cols = slice(v0 // STRIPE, (v0 + HALF) // STRIPE)
-            nc.vector.tensor_tensor(dst, y[i][:].indirect(offs[:, cols]), weight[:, v0 : v0 + HALF], ALU.mult)
+        def gather_weighted(dst, i, offs, weight, h):
+            nc.vector.tensor_tensor(dst, window(i, offs, h), weight[:, h * HALF : (h + 1) * HALF], ALU.mult)
 
-        def turn(term_r, term_l, dst):
-            turned = psum.tile([P, 2, P], F32, name="turned", bufs=2)
-            for i, term in enumerate((term_r, term_l)):
+        def gather_plain(dst, i, h):
+            nc.scalar.activation(dst, window(i, left_offs, h), ACT.Copy)
+
+        def turn(picked, b):
+            turned = bank(b, [P, 2, len(picked), P])
+            for a, term in enumerate(picked):
                 for c in range(2):
-                    nc.tensor.matmul(
-                        turned[:, c, :],
-                        term[:, c * P : (c + 1) * P],
-                        ident[:],
-                        start=(i, c) == (0, 0),
-                        stop=(i, c) == (1, 1),
-                        is_transpose=True,
-                    )
-            nc.scalar.copy(out=dst, in_=turned[:].rearrange("v c (t l) -> v c t l", l=dst.shape[3]))
+                    nc.tensor.transpose(turned[:, c, a, :], term[:, c * P : (c + 1) * P], ident[:])
+            return turned
 
-        def piece(i, v0, term_r, term_l, dst):
-            gather(term_r, right_offs, f_right, i, v0)
-            gather(term_l, left_offs, f_left, i, v0)
-            turn(term_r, term_l, dst)
-
-        def terms(name):
-            tile = sbuf(name, [P, 2, HALF], F32)
-            return tile[:, 0, :], tile[:, 1, :]
-
-        def turn_back(back, staging, t):
+        def weigh(name, turned, b0, back):
+            n = turned.shape[2]
+            staged = sbuf(name, [P, 2, n, P], F32)
             for c in range(2):
-                nc.tensor.transpose(back[:, t, c * P : (c + 1) * P], staging[:, c, t, :], ident[:])
+                nc.scalar.activation(staged[:, c], turned[:, c], ACT.Copy, scale=weights[:, b0 + c : b0 + c + 1])
+            for a in range(n):
+                for c in range(2):
+                    nc.tensor.transpose(back[:, a, c * P : (c + 1) * P], staged[:, c, a, :], ident[:])
 
         out_rows = out_0.rearrange("(p t) v -> p t v", t=PACK)
         out_words = out_1[0].rearrange("p n t -> p (n t)").bitcast(I32)
         o_scale = sbuf("o_scale", [P, T], U8)
-        o_bf = sbuf("o_bf", [P, T, PACK], BF16)
+        sums = [sbuf(f"sums{h}", [P, PACK, HALF], F32) for h in range(2)]
 
-        def round_sums(back, u, v0):
-            nc.scalar.copy(out=o_bf[:, v0 : v0 + HALF, 2 * u : 2 * u + 2], in_=back[:].rearrange("p t v -> p v t"))
+        def store_sums(u, h):
+            rows = slice(2 * u, 2 * u + 2)
+            nc.sync.dma_start(out=out_rows[:, rows, h * HALF : (h + 1) * HALF], in_=sums[h][:, rows, :])
 
-        def store_sums(back, u, v0, slot):
-            o = sbuf(slot, [P, 2, HALF], F32)
-            nc.scalar.copy(out=o[:], in_=back[:])
-            nc.sync.dma_start(out=out_rows[:, 2 * u : 2 * u + 2, v0 : v0 + HALF], in_=o[:])
-
-        round_w(nc.vector.tensor_copy, 0, 0, 0, WORDS)
-        round_w(nc.vector.tensor_copy, 0, 1, 0, WORDS // 2)
-        quantize_folded(0)
-        project(0, 0, HALF)
-        project(0, HALF, T)
-        round_w(nc.vector.tensor_copy, 0, 1, WORDS // 2, WORDS)
-        w_bf.append([sbuf(name, [P, 2, WORDS, PACK], BF16) for name in ("w_bf10", "w_scale0")])
-        quantize_plain(0)
-        round_w(nc.vector.tensor_copy, 1, 0, 0, WORDS)
-        quantize_folded(1)
-        project(1, 0, HALF)
-        project(1, HALF, T)
-        f_left = sbuf("w_codes0", [P, T], F32)
-        nc.scalar.activation(f_left[:], f_right[:], ACT.Copy, scale=-1.0, bias=1.0)
-        round_w(nc.scalar.copy, 1, 1, 0, WORDS)
-        first = [terms(f"terms{h}") for h in range(2)]
-        for h in range(2):
-            gather(first[h][0], right_offs, f_right, 0, h * HALF)
-        gather(first[0][1], left_offs, f_left, 0, 0)
-        quantize_plain(1)
-        project(2, 0, T)
-        project(3, 0, T)
-        gather(first[1][1], left_offs, f_left, 0, HALF)
-
-        staging = [sbuf(f"staging{i}", [P, 2, 2, P], F32) for i in range(3)]
-        backs = [psum.tile([P, 2, HALF], F32, name=f"back{i}") for i in range(3)]
-
-        for h in range(2):
-            turn(*first[h], staging[h][:, :, :, :WORDS])
-        for h in range(2):
-            piece(1, h * HALF, *terms(f"terms{2 + h}"), staging[h][:, :, :, WORDS:])
-        for t in range(2):
-            turn_back(backs[0], staging[0], t)
-        round_sums(backs[0], 0, 0)
-        piece(2, 0, *terms("terms4"), staging[2][:, :, 0:1, :])
-        store_sums(backs[0], 0, 0, "terms3")
-        piece(3, 0, *terms("terms5"), staging[2][:, :, 1:2, :])
-        for t in range(2):
-            turn_back(backs[2], staging[2], t)
-        for t in range(2):
-            turn_back(backs[1], staging[1], t)
-        store_sums(backs[2], 1, 0, "sums1")
-        round_sums(backs[2], 1, 0)
-        o = sbuf("staging1", [P, PACK, HALF], F32)
-        nc.scalar.copy(out=o[:, 0:2, :], in_=backs[1][:])
-        nc.sync.dma_start(out=out_rows[:, 0:2, HALF:], in_=o[:, 0:2, :])
-
-        def round_whole(copy, c0):
+        def round_sums(copy, h, c0, c1):
             copy(
-                out=o_bf[:, HALF + c0 : HALF + c0 + P, :].rearrange("p (c i) t -> p c t i", i=4),
-                in_=o[:, :, c0 : c0 + P].rearrange("p t (c i) -> p c t i", i=4),
+                out=o_bf[:, h * HALF + c0 : h * HALF + c1, :].rearrange("p (c i) t -> p c t i", i=4),
+                in_=sums[h][:, :, c0:c1].rearrange("p t (c i) -> p c t i", i=4),
             )
 
         def quantize_out(codes, v0, v1):
@@ -208,24 +152,84 @@ def tile_picked_wlerp_gelu_lo_kernel(
                 in_=o_bf[:, v0:v1, :].rearrange("p v t -> p (v t)"),
             )
 
-        last = [(f_right[:, :HALF], f_left[:, :HALF]), terms("terms4")]
+        low = round_w("w_low", 0, 0, PACK)
+        for t in range(PACK):
+            quantize_w(low[:, t], 0, t)
+        for u in range(2):
+            high = [round_w(f"w_high{e}", 1, 2 * u + e, 2 * u + e + 1) for e in range(2)]
+            for e in range(2):
+                quantize_w(high[e][:, 0], 1, 2 * u + e)
+        project(0, 0, HALF, 0)
+        project(0, HALF, T, 1)
+        for t in range(1, PACK):
+            project(t, 0, T, 1 + t)
+
+        f_left = sbuf("f_left", [P, T], F32)
+        nc.vector.tensor_scalar(f_left[:], f_right[:], -1.0, 1.0, ALU.mult, ALU.add)
+        rights = sbuf("rights", [P, 3, T], F32)
+        lefts = sbuf("lefts", [P, 2, HALF], F32)
+
+        def gather_right_whole(t):
+            nc.vector.tensor_tensor(rights[:, t, :], y[t][:].indirect(right_offs[:]), f_right[:], ALU.mult)
+
         for t in range(2):
-            gather(last[t][0], right_offs, f_right, 2 + t, HALF)
-            gather(last[t][1], left_offs, f_left, 2 + t, HALF)
-        nc.vector.tensor_tensor(o[:, 2, :], last[0][0], last[0][1], ALU.add)
+            gather_right_whole(t)
+            gather_weighted(lefts[:, t, :], t, left_offs, f_left, 0)
+        nc.vector.tensor_tensor(sums[0][:, 0:2, :], rights[:, 0:2, :HALF], lefts[:], ALU.add)
+        store_sums(0, 0)
+
+        early = sbuf("early", [P, 3, HALF], F32)
+        for a, (t, h) in enumerate(((2, 0), (3, 0), (0, 1))):
+            gather_plain(early[:, a, :], t, h)
+        frac_turned = bank(2, [P, PACK, P])
+        for b in range(PACK):
+            nc.tensor.transpose(frac_turned[:, b, :], f_right[:, b * P : (b + 1) * P], ident[:])
+        picked = sbuf("picked", [P, PACK, HALF], F32)
+        weights = picked[:, :, 0]
+        nc.scalar.activation(weights, frac_turned[:, :, 0], ACT.Copy, scale=-1.0, bias=1.0)
+        back_0 = bank(5, [P, 2, HALF])
+        weigh("staged0", turn([early[:, 0, :], early[:, 1, :]], 0), 0, back_0)
+        back_1 = [bank(b, [P, 1, HALF]) for b in (6, 7, 0)]
+        turned = turn([early[:, 2, :]], 1)
+        gather_plain(picked[:, 0, :], 1, 1)
+        turned_next = turn([picked[:, 0, :]], 3)
+        weigh("staged1", turned, 2, back_1[0])
+        left_2 = sbuf("staged0", [P, HALF], F32)
+        gather_plain(left_2[:], 2, 1)
+        turned = turn([left_2[:]], 4)
+        weigh("staged2", turned_next, 2, back_1[1])
+        left_3 = sbuf("staged1", [P, HALF], F32)
+        gather_plain(left_3[:], 3, 1)
+        weigh("staged3", turned, 2, back_1[2])
+        back_2 = back_1[2]
+        o_bf = sbuf("staged2", [P, T, PACK], BF16)
+
+        gather_right_whole(2)
+        right_3 = sbuf("right_3", [P, HALF], F32)
+        gather_weighted(right_3[:], 3, right_offs, f_right, 0)
+        right_last, left_last = rights[:, 2, :HALF], right_3[:]
+        for t, term in enumerate((right_last, left_last)):
+            nc.vector.tensor_tensor(sums[0][:, 2 + t, :], back_0[:, t, :], term, ALU.add)
+        store_sums(1, 0)
+        gather_weighted(right_last, 3, right_offs, f_right, 1)
+        round_sums(nc.scalar.copy, 0, 0, HALF)
+        for t in range(2):
+            nc.vector.tensor_tensor(sums[1][:, t, :], back_1[t][:, 0, :], rights[:, t, HALF:], ALU.add)
+        store_sums(0, 1)
+        nc.vector.tensor_tensor(left_last, left_3[:], f_left[:, HALF:], ALU.mult)
         for c0 in (0, P):
             cols = slice(c0, c0 + P)
-            nc.vector.tensor_tensor(o[:, 3, cols], last[1][0][:, cols], last[1][1][:, cols], ALU.add)
-        nc.sync.dma_start(out=out_rows[:, 2:4, HALF:], in_=o[:, 2:4, :])
-        round_whole(nc.scalar.copy, P)
-        codes = sbuf("f_right", [P, HALF], U32)
-        quantize_out(codes[:], 0, HALF)
-        nc.sync.dma_start(out=out_words[:, :HALF], in_=codes[:].bitcast(I32))
-        round_whole(nc.vector.tensor_copy, 0)
-        codes = sbuf("codes", [P, HALF], U32)
+            nc.vector.tensor_tensor(sums[1][:, 2, cols], back_2[:, 0, cols], rights[:, 2, HALF + c0 : HALF + c0 + P], ALU.add)
+            nc.vector.tensor_tensor(sums[1][:, 3, cols], left_last[:, cols], right_last[:, cols], ALU.add)
+        store_sums(1, 1)
+        round_sums(nc.scalar.copy, 1, P, HALF)
+        round_sums(nc.vector.tensor_copy, 1, 0, P)
+        codes = [sbuf(f"codes{h}", [P, HALF], U32) for h in range(2)]
+        quantize_out(codes[0][:], 0, HALF)
+        nc.sync.dma_start(out=out_words[:, :HALF], in_=codes[0][:].bitcast(I32))
         for c0 in (0, P):
-            quantize_out(codes[:, c0 : c0 + P], HALF + c0, HALF + c0 + P)
-        nc.sync.dma_start(out=out_words[:, HALF:], in_=codes[:].bitcast(I32))
+            quantize_out(codes[1][:, c0 : c0 + P], HALF + c0, HALF + c0 + P)
+        nc.sync.dma_start(out=out_words[:, HALF:], in_=codes[1][:].bitcast(I32))
 
         for q in range(4):
             queue = nc.scalar if q % 2 else nc.sync

@@ -36,7 +36,7 @@ def tile_picked_wlerp_gelu_lo_kernel(
             return keep.tile(shape, dtype, name=name, align_bytes=64)
 
         w_rows = w1.rearrange("(p j) m -> p j m", j=PACK)
-        w_raw = [sbuf(f"w_raw{s}", [P, PACK, N // 2], F32) for s in range(2)]
+        w_raw = [sbuf(f"w_raw{s}", [P, 2, N], F32) for s in range(2)]
         x_codes = sbuf("x_codes", [P, T], U32)
         x_scale = sbuf("x_scale", [P, T], U8)
         f_right = sbuf("f_right", [P, T], F32)
@@ -49,10 +49,10 @@ def tile_picked_wlerp_gelu_lo_kernel(
                 in_=x_scales[0, 4 * q : 4 * q + 4, :].bitcast(I32),
             )
 
-        nc.sync.dma_start(out=w_raw[0][:], in_=w_rows[:, :, : N // 2])
+        nc.sync.dma_start(out=w_raw[0][:], in_=w_rows[:, 0:2, :])
         for q in range(4):
             load_scales(nc.scalar if q < 3 else nc.sync, q)
-        nc.sync.dma_start(out=w_raw[1][:], in_=w_rows[:, :, N // 2 :])
+        nc.sync.dma_start(out=w_raw[1][:], in_=w_rows[:, 2:4, :])
         nc.sync.dma_start(
             out=x_codes[:].bitcast(I32),
             in_=x_words[0].rearrange("p n t -> p (n t)").bitcast(I32),
@@ -73,20 +73,19 @@ def tile_picked_wlerp_gelu_lo_kernel(
             nc.gpsimd.memset(y[i][:, T:], 0.0)
         w_codes = [sbuf(f"w_codes{t}", [P, P], U32) for t in range(PACK)]
         w_scale = [sbuf(f"w_scale{t}", [P, P], U8) for t in range(PACK)]
-        def round_w(name, s, t0, t1):
-            dst = sbuf(name, [P, t1 - t0, WORDS, PACK], BF16)
-            nc.vector.tensor_copy(
-                out=dst[:].rearrange("p t l j -> p l t j"),
+        w_bf = sbuf("w_bf", [P, PACK, P, PACK], BF16)
+
+        def round_w(copy, s, t0, t1):
+            copy(
+                out=w_bf[:, t0:t1, :, 2 * s : 2 * s + 2].rearrange("p t l j -> p l t j"),
                 in_=w_raw[s][:].rearrange("p j (l t) -> p l t j", t=PACK)[:, :, t0:t1, :],
             )
-            return dst
 
-        def quantize_w(src, s, t):
-            words = slice(s * WORDS, (s + 1) * WORDS)
+        def quantize_w(t):
             nc.vector.quantize_mx(
-                out=w_codes[t][:, words].bitcast(FP8X4),
-                scales=w_scale[t][:, words],
-                in_=src.rearrange("p l j -> p (l j)"),
+                out=w_codes[t][:].bitcast(FP8X4),
+                scales=w_scale[t][:],
+                in_=w_bf[:, t].rearrange("p l j -> p (l j)"),
             )
 
         def bank(b, shape):
@@ -152,13 +151,12 @@ def tile_picked_wlerp_gelu_lo_kernel(
                 in_=o_bf[:, v0:v1, :].rearrange("p v t -> p (v t)"),
             )
 
-        low = round_w("w_low", 0, 0, PACK)
+        round_w(nc.vector.tensor_copy, 0, 0, PACK)
+        for t in range(2):
+            round_w(nc.vector.tensor_copy, 1, t, t + 1)
+        round_w(nc.scalar.copy, 1, 2, PACK)
         for t in range(PACK):
-            quantize_w(low[:, t], 0, t)
-        for u in range(2):
-            high = [round_w(f"w_high{e}", 1, 2 * u + e, 2 * u + e + 1) for e in range(2)]
-            for e in range(2):
-                quantize_w(high[e][:, 0], 1, 2 * u + e)
+            quantize_w(t)
         project(0, 0, HALF, 0)
         project(0, HALF, T, 1)
         for t in range(1, PACK):

@@ -192,9 +192,8 @@ def tile_picked_wlerp_gelu_lo_kernel(
         gather_plain(picked[:, 0, :], 1, 1)
         turned_next = turn([picked[:, 0, :]], 3)
         weigh("staged1", turned, 2, back_1[0])
-        left_2 = sbuf("staged0", [P, HALF], F32)
-        gather_plain(left_2[:], 2, 1)
-        turned = turn([left_2[:]], 4)
+        gather_plain(picked[:, 1, :], 2, 1)
+        turned = turn([picked[:, 1, :]], 4)
         weigh("staged2", turned_next, 2, back_1[1])
         left_3 = sbuf("staged1", [P, HALF], F32)
         gather_plain(left_3[:], 3, 1)
@@ -211,21 +210,21 @@ def tile_picked_wlerp_gelu_lo_kernel(
         store_sums(1, 0)
         gather_weighted(right_last, 3, right_offs, f_right, 1)
         round_sums(nc.scalar.copy, 0, 0, HALF)
-        for t in range(2):
-            nc.vector.tensor_tensor(sums[1][:, t, :], back_1[t][:, 0, :], rights[:, t, HALF:], ALU.add)
-        store_sums(0, 1)
+        nc.vector.tensor_tensor(sums[1][:, 0, :], back_1[0][:, 0, :], rights[:, 0, HALF:], ALU.add)
         nc.vector.tensor_tensor(left_last, left_3[:], f_left[:, HALF:], ALU.mult)
-        for c0 in (0, P):
+        nc.vector.tensor_tensor(sums[1][:, 1, :], back_1[1][:, 0, :], rights[:, 1, HALF:], ALU.add)
+        store_sums(0, 1)
+        nc.vector.tensor_tensor(sums[1][:, 3, :], left_last, right_last, ALU.add)
+        for c0 in (P, 0):
             cols = slice(c0, c0 + P)
             nc.vector.tensor_tensor(sums[1][:, 2, cols], back_2[:, 0, cols], rights[:, 2, HALF + c0 : HALF + c0 + P], ALU.add)
-            nc.vector.tensor_tensor(sums[1][:, 3, cols], left_last[:, cols], right_last[:, cols], ALU.add)
         store_sums(1, 1)
         round_sums(nc.scalar.copy, 1, P, HALF)
-        round_sums(nc.vector.tensor_copy, 1, 0, P)
         codes = [sbuf(f"codes{h}", [P, HALF], U32) for h in range(2)]
         quantize_out(codes[0][:], 0, HALF)
         nc.sync.dma_start(out=out_words[:, :HALF], in_=codes[0][:].bitcast(I32))
-        for c0 in (0, P):
+        round_sums(nc.vector.tensor_copy, 1, 0, P)
+        for c0 in (P, 0):
             quantize_out(codes[1][:, c0 : c0 + P], HALF + c0, HALF + c0 + P)
         nc.sync.dma_start(out=out_words[:, HALF:], in_=codes[1][:].bitcast(I32))
 

@@ -33,7 +33,7 @@ def tile_picked_wlerp_gelu_lo_kernel(
         psum = ctx.enter_context(tc.psum_pool(name="psum", bufs=1))
 
         def sbuf(name, shape, dtype):
-            return keep.tile(shape, dtype, name=name, align_bytes=64)
+            return keep.tile(shape, dtype, name=name, align_bytes=256)
 
         w_rows = w1.rearrange("(p j) m -> p j m", j=PACK)
         w_raw = [sbuf(f"w_raw{s}", [P, 2, N], F32) for s in range(2)]
@@ -151,10 +151,11 @@ def tile_picked_wlerp_gelu_lo_kernel(
                 in_=o_bf[:, v0:v1, :].rearrange("p v t -> p (v t)"),
             )
 
-        round_w(nc.vector.tensor_copy, 0, 0, PACK)
+        round_w(nc.vector.tensor_copy, 0, 0, 2)
         for t in range(2):
             round_w(nc.vector.tensor_copy, 1, t, t + 1)
-        round_w(nc.scalar.copy, 1, 2, PACK)
+        for s in range(2):
+            round_w(nc.scalar.copy, s, 2, PACK)
         for t in range(PACK):
             quantize_w(t)
         project(0, 0, HALF, 0)

@@ -60,6 +60,9 @@ def tile_picked_wlerp_gelu_lo_kernel(
         nc.sync.dma_start(right_offs[:], right)
         nc.sync.dma_start(out=f_right[:], in_=frac)
         nc.sync.dma_start(left_offs[:], left)
+        early = sbuf("early", [P, 4, HALF], F32)
+        f_blocks = early[:, 3, :P]
+        nc.sync.dma_start(out=f_blocks, in_=frac.rearrange("r (b i) -> (r b) i", b=PACK)[:P, :])
 
         ident = sbuf("ident", [P, P], F32)
         make_identity(nc, ident[:])
@@ -125,8 +128,8 @@ def tile_picked_wlerp_gelu_lo_kernel(
             staged = sbuf(name, [P, 2, n, P], F32)
             for c in range(2):
                 nc.scalar.activation(staged[:, c], turned[:, c], ACT.Copy, scale=weights[:, b0 + c : b0 + c + 1])
-            for a in range(n):
-                for c in range(2):
+            for c in range(2):
+                for a in range(n):
                     nc.tensor.transpose(back[:, a, c * P : (c + 1) * P], staged[:, c, a, :], ident[:])
 
         out_rows = out_0.rearrange("(p t) v -> p t v", t=PACK)
@@ -174,54 +177,49 @@ def tile_picked_wlerp_gelu_lo_kernel(
         for t in range(2):
             gather_right_whole(t)
             gather_weighted(lefts[:, t, :], t, left_offs, f_left, 0)
-        nc.vector.tensor_tensor(sums[0][:, 0:2, :], rights[:, 0:2, :HALF], lefts[:], ALU.add)
-        store_sums(0, 0)
 
-        early = sbuf("early", [P, 3, HALF], F32)
         for a, (t, h) in enumerate(((2, 0), (3, 0), (0, 1))):
             gather_plain(early[:, a, :], t, h)
-        frac_turned = bank(2, [P, PACK, P])
-        for b in range(PACK):
-            nc.tensor.transpose(frac_turned[:, b, :], f_right[:, b * P : (b + 1) * P], ident[:])
-        picked = sbuf("picked", [P, PACK, HALF], F32)
-        weights = picked[:, :, 0]
-        nc.scalar.activation(weights, frac_turned[:, :, 0], ACT.Copy, scale=-1.0, bias=1.0)
+        frac_turned = bank(2, [P, P])
+        nc.tensor.transpose(frac_turned[:], f_blocks, ident[:])
+        weights = sbuf("weights", [P, PACK], F32)
+        nc.scalar.activation(weights[:], frac_turned[:, :PACK], ACT.Copy, scale=-1.0, bias=1.0)
+        gather_plain(early[:, 3, :], 1, 1)
         back_0 = bank(5, [P, 2, HALF])
-        weigh("staged0", turn([early[:, 0, :], early[:, 1, :]], 0), 0, back_0)
-        back_1 = [bank(b, [P, 1, HALF]) for b in (6, 7, 0)]
-        turned = turn([early[:, 2, :]], 1)
-        gather_plain(picked[:, 0, :], 1, 1)
-        turned_next = turn([picked[:, 0, :]], 3)
-        weigh("staged1", turned, 2, back_1[0])
-        gather_plain(picked[:, 1, :], 2, 1)
-        turned = turn([picked[:, 1, :]], 4)
-        weigh("staged2", turned_next, 2, back_1[1])
-        left_3 = sbuf("staged1", [P, HALF], F32)
-        gather_plain(left_3[:], 3, 1)
-        weigh("staged3", turned, 2, back_1[2])
-        back_2 = back_1[2]
-        o_bf = sbuf("staged2", [P, T, PACK], BF16)
+        turned_first = turn([early[:, 0, :], early[:, 1, :]], 0)
+        turned_second = turn([early[:, 2, :], early[:, 3, :]], 1)
+        weigh("staged0", turned_first, 0, back_0)
+        gather_plain(early[:, 1, :], 2, 1)
+        turned_last = turn([early[:, 1, :]], 4)
+        back_1 = bank(6, [P, 2, HALF])
+        weigh("staged1", turned_second, 2, back_1)
+        left_3 = early[:, 3, :]
+        gather_plain(left_3, 3, 1)
+        back_2 = bank(7, [P, 1, HALF])
+        weigh("staged3", turned_last, 2, back_2)
+        o_bf = sbuf("staged1", [P, T, PACK], BF16)
 
         gather_right_whole(2)
         right_3 = sbuf("right_3", [P, HALF], F32)
         gather_weighted(right_3[:], 3, right_offs, f_right, 0)
+        nc.vector.tensor_tensor(sums[0][:, 0:2, :], rights[:, 0:2, :HALF], lefts[:], ALU.add)
+        store_sums(0, 0)
         right_last, left_last = rights[:, 2, :HALF], right_3[:]
         for t, term in enumerate((right_last, left_last)):
             nc.vector.tensor_tensor(sums[0][:, 2 + t, :], back_0[:, t, :], term, ALU.add)
         store_sums(1, 0)
         gather_weighted(right_last, 3, right_offs, f_right, 1)
         round_sums(nc.scalar.copy, 0, 0, HALF)
-        nc.vector.tensor_tensor(sums[1][:, 0, :], back_1[0][:, 0, :], rights[:, 0, HALF:], ALU.add)
-        nc.vector.tensor_tensor(left_last, left_3[:], f_left[:, HALF:], ALU.mult)
-        nc.vector.tensor_tensor(sums[1][:, 1, :], back_1[1][:, 0, :], rights[:, 1, HALF:], ALU.add)
+        nc.gpsimd.tensor_tensor(left_last, left_3, f_left[:, HALF:], ALU.mult)
+        nc.vector.tensor_tensor(sums[1][:, 0:2, :], back_1[:], rights[:, 0:2, HALF:], ALU.add)
         store_sums(0, 1)
-        nc.vector.tensor_tensor(sums[1][:, 3, :], left_last, right_last, ALU.add)
+        nc.vector.tensor_tensor(sums[1][:, 2, :], back_2[:, 0, :], rights[:, 2, HALF:], ALU.add)
         for c0 in (P, 0):
             cols = slice(c0, c0 + P)
-            nc.vector.tensor_tensor(sums[1][:, 2, cols], back_2[:, 0, cols], rights[:, 2, HALF + c0 : HALF + c0 + P], ALU.add)
+            nc.vector.tensor_tensor(sums[1][:, 3, cols], left_last[:, cols], right_last[:, cols], ALU.add)
         store_sums(1, 1)
         round_sums(nc.scalar.copy, 1, P, HALF)
-        codes = [sbuf(f"codes{h}", [P, HALF], U32) for h in range(2)]
+        codes = [sbuf(name, [P, HALF], U32) for name in ("staged3", "codes1")]
         quantize_out(codes[0][:], 0, HALF)
         nc.sync.dma_start(out=out_words[:, :HALF], in_=codes[0][:].bitcast(I32))
         round_sums(nc.vector.tensor_copy, 1, 0, P)

@@ -71,8 +71,8 @@ def tile_picked_wlerp_gelu_lo_kernel(
         warm = sbuf("warm", [P, SPARE], F32)
         nc.scalar.activation(warm[:], zeros[:], ACT.Gelu_apprx_tanh)
 
-        y = [sbuf(f"y{i}", [P, T + SPARE if i < 3 else T], F32) for i in range(4)]
-        for i in range(3):
+        y = [sbuf(f"y{i}", [P, T + SPARE if i < 2 else T], F32) for i in range(4)]
+        for i in range(2):
             nc.gpsimd.memset(y[i][:, T:], 0.0)
         w_codes = [sbuf(f"w_codes{t}", [P, P], U32) for t in range(PACK)]
         w_scale = [sbuf(f"w_scale{t}", [P, P], U8) for t in range(PACK)]
@@ -168,7 +168,7 @@ def tile_picked_wlerp_gelu_lo_kernel(
 
         f_left = sbuf("f_left", [P, T], F32)
         nc.vector.tensor_scalar(f_left[:], f_right[:], -1.0, 1.0, ALU.mult, ALU.add)
-        rights = sbuf("rights", [P, 3, T], F32)
+        rights = sbuf("rights", [P, PACK, T], F32)
         lefts = sbuf("lefts", [P, 2, HALF], F32)
 
         def gather_right_whole(t):
@@ -199,15 +199,14 @@ def tile_picked_wlerp_gelu_lo_kernel(
         weigh("staged3", turned_last, 2, back_2)
         o_bf = sbuf("staged1", [P, T, PACK], BF16)
 
-        gather_right_whole(2)
-        right_3 = sbuf("right_3", [P, HALF], F32)
-        gather_weighted(right_3[:], 3, right_offs, f_right, 0)
+        gather_weighted(rights[:, 2, :HALF], 2, right_offs, f_right, 0)
         nc.vector.tensor_tensor(sums[0][:, 0:2, :], rights[:, 0:2, :HALF], lefts[:], ALU.add)
         store_sums(0, 0)
-        right_last, left_last = rights[:, 2, :HALF], right_3[:]
-        for t, term in enumerate((right_last, left_last)):
-            nc.vector.tensor_tensor(sums[0][:, 2 + t, :], back_0[:, t, :], term, ALU.add)
+        gather_weighted(rights[:, 3, :HALF], 3, right_offs, f_right, 0)
+        gather_weighted(rights[:, 2, HALF:], 2, right_offs, f_right, 1)
+        nc.vector.tensor_tensor(sums[0][:, 2:4, :], back_0[:], rights[:, 2:4, :HALF], ALU.add)
         store_sums(1, 0)
+        right_last, left_last = sbuf("staged0", [P, HALF], F32)[:], rights[:, 3, :HALF]
         gather_weighted(right_last, 3, right_offs, f_right, 1)
         round_sums(nc.scalar.copy, 0, 0, HALF)
         nc.gpsimd.tensor_tensor(left_last, left_3, f_left[:, HALF:], ALU.mult)

@@ -71,8 +71,8 @@ def tile_picked_wlerp_gelu_lo_kernel(
         warm = sbuf("warm", [P, SPARE], F32)
         nc.scalar.activation(warm[:], zeros[:], ACT.Gelu_apprx_tanh)
 
-        y = [sbuf(f"y{i}", [P, T + SPARE if i < 2 else T], F32) for i in range(4)]
-        for i in range(2):
+        y = [sbuf(f"y{i}", [P, T + SPARE if i < 3 else T], F32) for i in range(4)]
+        for i in range(3):
             nc.gpsimd.memset(y[i][:, T:], 0.0)
         w_codes = [sbuf(f"w_codes{t}", [P, P], U32) for t in range(PACK)]
         w_scale = [sbuf(f"w_scale{t}", [P, P], U8) for t in range(PACK)]
@@ -199,11 +199,10 @@ def tile_picked_wlerp_gelu_lo_kernel(
         weigh("staged3", turned_last, 2, back_2)
         o_bf = sbuf("staged1", [P, T, PACK], BF16)
 
-        gather_weighted(rights[:, 2, :HALF], 2, right_offs, f_right, 0)
+        gather_right_whole(2)
+        gather_weighted(rights[:, 3, :HALF], 3, right_offs, f_right, 0)
         nc.vector.tensor_tensor(sums[0][:, 0:2, :], rights[:, 0:2, :HALF], lefts[:], ALU.add)
         store_sums(0, 0)
-        gather_weighted(rights[:, 3, :HALF], 3, right_offs, f_right, 0)
-        gather_weighted(rights[:, 2, HALF:], 2, right_offs, f_right, 1)
         nc.vector.tensor_tensor(sums[0][:, 2:4, :], back_0[:], rights[:, 2:4, :HALF], ALU.add)
         store_sums(1, 0)
         right_last, left_last = sbuf("staged0", [P, HALF], F32)[:], rights[:, 3, :HALF]

@@ -123,14 +123,13 @@ def tile_picked_wlerp_gelu_lo_kernel(
                     nc.tensor.transpose(turned[:, c, a, :], term[:, c * P : (c + 1) * P], ident[:])
             return turned
 
-        def weigh(name, turned, b0, back):
+        def weigh(staged, turned, b0, back):
             n = turned.shape[2]
-            staged = sbuf(name, [P, 2, n, P], F32)
             for c in range(2):
                 nc.scalar.activation(staged[:, c], turned[:, c], ACT.Copy, scale=weights[:, b0 + c : b0 + c + 1])
             for c in range(2):
                 for a in range(n):
-                    nc.tensor.transpose(back[:, a, c * P : (c + 1) * P], staged[:, c, a, :], ident[:])
+                    nc.tensor.transpose(back[c][:, a, :], staged[:, c, a, :], ident[:])
 
         out_rows = out_0.rearrange("(p t) v -> p t v", t=PACK)
         out_words = out_1[0].rearrange("p n t -> p (n t)").bitcast(I32)
@@ -185,39 +184,46 @@ def tile_picked_wlerp_gelu_lo_kernel(
         weights = sbuf("weights", [P, PACK], F32)
         nc.scalar.activation(weights[:], frac_turned[:, :PACK], ACT.Copy, scale=-1.0, bias=1.0)
         gather_plain(early[:, 3, :], 1, 1)
-        back_0 = bank(5, [P, 2, HALF])
+        back_0 = [bank(b, [P, 2, P]) for b in (5, 3)]
         turned_first = turn([early[:, 0, :], early[:, 1, :]], 0)
         turned_second = turn([early[:, 2, :], early[:, 3, :]], 1)
-        weigh("staged0", turned_first, 0, back_0)
+        weigh(sbuf("staged0", [P, 2, 2, P], F32), turned_first, 0, back_0)
         gather_plain(early[:, 1, :], 2, 1)
         turned_last = turn([early[:, 1, :]], 4)
         back_1 = bank(6, [P, 2, HALF])
-        weigh("staged1", turned_second, 2, back_1)
+        weigh(sbuf("staged1", [P, 2, 2, P], F32), turned_second, 2, [back_1[:, :, c * P : (c + 1) * P] for c in range(2)])
         left_3 = early[:, 3, :]
         gather_plain(left_3, 3, 1)
         back_2 = bank(7, [P, 1, HALF])
-        weigh("staged3", turned_last, 2, back_2)
+        weigh(sums[1][:, 3, :].rearrange("p (c a i) -> p c a i", c=2, a=1), turned_last, 2, [back_2[:, :, c * P : (c + 1) * P] for c in range(2)])
         o_bf = sbuf("staged1", [P, T, PACK], BF16)
 
         gather_right_whole(2)
         gather_weighted(rights[:, 3, :HALF], 3, right_offs, f_right, 0)
         nc.vector.tensor_tensor(sums[0][:, 0:2, :], rights[:, 0:2, :HALF], lefts[:], ALU.add)
         store_sums(0, 0)
-        nc.vector.tensor_tensor(sums[0][:, 2:4, :], back_0[:], rights[:, 2:4, :HALF], ALU.add)
-        store_sums(1, 0)
-        right_last, left_last = sbuf("staged0", [P, HALF], F32)[:], rights[:, 3, :HALF]
+        nc.vector.tensor_tensor(sums[0][:, 2:4, :P], back_0[0][:], rights[:, 2:4, :P], ALU.add)
+        right_last, left_last = sbuf("staged0", [P, HALF], F32)[:], rights[:, 2:4, :P]
         gather_weighted(right_last, 3, right_offs, f_right, 1)
-        round_sums(nc.scalar.copy, 0, 0, HALF)
-        nc.gpsimd.tensor_tensor(left_last, left_3, f_left[:, HALF:], ALU.mult)
+        nc.vector.tensor_tensor(sums[0][:, 2:4, P:], back_0[1][:], rights[:, 2:4, P:HALF], ALU.add)
+        store_sums(1, 0)
+        for c0 in (0, P):
+            round_sums(nc.scalar.copy, 0, c0, c0 + P)
+        nc.gpsimd.tensor_tensor(
+            left_last,
+            left_3.rearrange("p (c i) -> p c i", c=2),
+            f_left[:, HALF:].rearrange("p (c i) -> p c i", c=2),
+            ALU.mult,
+        )
         nc.vector.tensor_tensor(sums[1][:, 0:2, :], back_1[:], rights[:, 0:2, HALF:], ALU.add)
         store_sums(0, 1)
         nc.vector.tensor_tensor(sums[1][:, 2, :], back_2[:, 0, :], rights[:, 2, HALF:], ALU.add)
         for c0 in (P, 0):
             cols = slice(c0, c0 + P)
-            nc.vector.tensor_tensor(sums[1][:, 3, cols], left_last[:, cols], right_last[:, cols], ALU.add)
+            nc.vector.tensor_tensor(sums[1][:, 3, cols], left_last[:, c0 // P, :], right_last[:, cols], ALU.add)
         store_sums(1, 1)
         round_sums(nc.scalar.copy, 1, P, HALF)
-        codes = [sbuf(name, [P, HALF], U32) for name in ("staged3", "codes1")]
+        codes = [sbuf(name, [P, HALF], U32) for name in ("codes0", "codes1")]
         quantize_out(codes[0][:], 0, HALF)
         nc.sync.dma_start(out=out_words[:, :HALF], in_=codes[0][:].bitcast(I32))
         round_sums(nc.vector.tensor_copy, 1, 0, P)

@@ -71,8 +71,8 @@ def tile_picked_wlerp_gelu_lo_kernel(
         warm = sbuf("warm", [P, SPARE], F32)
         nc.scalar.activation(warm[:], zeros[:], ACT.Gelu_apprx_tanh)
 
-        y = [sbuf(f"y{i}", [P, T + SPARE if i < 3 else T], F32) for i in range(4)]
-        for i in range(3):
+        y = [sbuf(f"y{i}", [P, T + SPARE], F32) for i in range(4)]
+        for i in range(PACK):
             nc.gpsimd.memset(y[i][:, T:], 0.0)
         w_codes = [sbuf(f"w_codes{t}", [P, P], U32) for t in range(PACK)]
         w_scale = [sbuf(f"w_scale{t}", [P, P], U8) for t in range(PACK)]
@@ -198,29 +198,23 @@ def tile_picked_wlerp_gelu_lo_kernel(
         weigh(sums[1][:, 3, :].rearrange("p (c a i) -> p c a i", c=2, a=1), turned_last, 2, [back_2[:, :, c * P : (c + 1) * P] for c in range(2)])
         o_bf = sbuf("staged1", [P, T, PACK], BF16)
 
-        gather_right_whole(2)
-        gather_weighted(rights[:, 3, :HALF], 3, right_offs, f_right, 0)
+        for t in (2, 3):
+            gather_right_whole(t)
         nc.vector.tensor_tensor(sums[0][:, 0:2, :], rights[:, 0:2, :HALF], lefts[:], ALU.add)
         store_sums(0, 0)
         nc.vector.tensor_tensor(sums[0][:, 2:4, :P], back_0[0][:], rights[:, 2:4, :P], ALU.add)
-        right_last, left_last = sbuf("staged0", [P, HALF], F32)[:], rights[:, 2:4, :P]
-        gather_weighted(right_last, 3, right_offs, f_right, 1)
+        right_last, left_last = rights[:, 3, HALF:], lefts[:, 0, :]
         nc.vector.tensor_tensor(sums[0][:, 2:4, P:], back_0[1][:], rights[:, 2:4, P:HALF], ALU.add)
         store_sums(1, 0)
         for c0 in (0, P):
             round_sums(nc.scalar.copy, 0, c0, c0 + P)
-        nc.gpsimd.tensor_tensor(
-            left_last,
-            left_3.rearrange("p (c i) -> p c i", c=2),
-            f_left[:, HALF:].rearrange("p (c i) -> p c i", c=2),
-            ALU.mult,
-        )
+        nc.gpsimd.tensor_tensor(left_last, left_3, f_left[:, HALF:], ALU.mult)
         nc.vector.tensor_tensor(sums[1][:, 0:2, :], back_1[:], rights[:, 0:2, HALF:], ALU.add)
         store_sums(0, 1)
         nc.vector.tensor_tensor(sums[1][:, 2, :], back_2[:, 0, :], rights[:, 2, HALF:], ALU.add)
         for c0 in (P, 0):
             cols = slice(c0, c0 + P)
-            nc.vector.tensor_tensor(sums[1][:, 3, cols], left_last[:, c0 // P, :], right_last[:, cols], ALU.add)
+            nc.vector.tensor_tensor(sums[1][:, 3, cols], left_last[:, cols], right_last[:, cols], ALU.add)
         store_sums(1, 1)
         round_sums(nc.scalar.copy, 1, P, HALF)
         codes = [sbuf(name, [P, HALF], U32) for name in ("codes0", "codes1")]

@@ -51,7 +51,7 @@ def tile_picked_wlerp_gelu_lo_kernel(
 
         nc.sync.dma_start(out=w_raw[0][:], in_=w_rows[:, 0:2, :])
         for q in range(4):
-            load_scales(nc.scalar if q < 3 else nc.sync, q)
+            load_scales(nc.scalar, q)
         nc.sync.dma_start(out=w_raw[1][:], in_=w_rows[:, 2:4, :])
         nc.sync.dma_start(
             out=x_codes[:].bitcast(I32),

from contextlib import ExitStack

import concourse.mybir as mybir
from concourse.masks import make_identity

K, T, N = 512, 512, 512
FLOPS = 2 * K * T * N

F32 = mybir.dt.float32
BF16 = mybir.dt.bfloat16
I32 = mybir.dt.int32
U32 = mybir.dt.uint32
U16 = mybir.dt.uint16
U8 = mybir.dt.uint8
FP8X4 = mybir.dt.float8_e4m3fn_x4
ALU = mybir.AluOpType
ACT = mybir.ActivationFunctionType

P = 128
PACK = 4
STRIPE = 16
HALF = T // 2
WORDS = P // 2
SPARE = 16


def tile_picked_wlerp_gelu_lo_kernel(
    tc, x_words, x_scales, w1, frac, left, right, out_0, out_1, out_2
):
    nc = tc.nc
    with ExitStack() as ctx:
        keep = ctx.enter_context(tc.tile_pool(name="keep", bufs=1))
        psum = ctx.enter_context(tc.psum_pool(name="psum", bufs=1))

        def sbuf(name, shape, dtype):
            return keep.tile(shape, dtype, name=name, align_bytes=256)

        w_rows = w1.rearrange("(p j) m -> p j m", j=PACK)
        w_raw = [sbuf(f"w_raw{s}", [P, 2, N], F32) for s in range(2)]
        x_codes = sbuf("x_codes", [P, T], U32)
        x_scale = sbuf("x_scale", [P, T], U8)
        f_right = sbuf("f_right", [P, T], F32)
        right_offs = keep.tile([P, T // STRIPE], U16, name="right_offs")
        left_offs = keep.tile([P, T // STRIPE], U16, name="left_offs")

        def load_scales(queue, q):
            queue.dma_start(
                out=x_scale[32 * q : 32 * q + 4, :].bitcast(I32),
                in_=x_scales[0, 4 * q : 4 * q + 4, :].bitcast(I32),
            )

        nc.sync.dma_start(out=w_raw[0][:], in_=w_rows[:, 0:2, :])
        for q in range(4):
            load_scales(nc.scalar, q)
        nc.sync.dma_start(out=w_raw[1][:], in_=w_rows[:, 2:4, :])
        nc.sync.dma_start(
            out=x_codes[:].bitcast(I32),
            in_=x_words[0].rearrange("p n t -> p (n t)").bitcast(I32),
        )
        nc.sync.dma_start(right_offs[:], right)
        nc.sync.dma_start(out=f_right[:], in_=frac)
        nc.sync.dma_start(left_offs[:], left)
        early = sbuf("early", [P, 4, HALF], F32)
        f_blocks = early[:, 3, :P]
        nc.sync.dma_start(out=f_blocks, in_=frac.rearrange("r (b i) -> (r b) i", b=PACK)[:P, :])

        ident = sbuf("ident", [P, P], F32)
        make_identity(nc, ident[:])
        zeros = sbuf("zeros", [P, SPARE], F32)
        nc.vector.memset(zeros[:], 0.0)
        warm = sbuf("warm", [P, SPARE], F32)
        nc.scalar.activation(warm[:], zeros[:], ACT.Gelu_apprx_tanh)

        y = [sbuf(f"y{i}", [P, T + SPARE], F32) for i in range(4)]
        for i in range(PACK):
            nc.gpsimd.memset(y[i][:, T:], 0.0)
        w_codes = [sbuf(f"w_codes{t}", [P, P], U32) for t in range(PACK)]
        w_scale = [sbuf(f"w_scale{t}", [P, P], U8) for t in range(PACK)]
        w_bf = sbuf("w_bf", [P, PACK, P, PACK], BF16)

        def round_w(copy, s, t0, t1):
            copy(
                out=w_bf[:, t0:t1, :, 2 * s : 2 * s + 2].rearrange("p t l j -> p l t j"),
                in_=w_raw[s][:].rearrange("p j (l t) -> p l t j", t=PACK)[:, :, t0:t1, :],
            )

        def quantize_w(t):
            nc.vector.quantize_mx(
                out=w_codes[t][:].bitcast(FP8X4),
                scales=w_scale[t][:],
                in_=w_bf[:, t].rearrange("p l j -> p (l j)"),
            )

        def bank(b, shape):
            return psum.tile(shape, F32, name=f"bank{b}")

        def project(i, c0, c1, b):
            acc = bank(b, [P, c1 - c0])
            nc.tensor.matmul_mx(
                out=acc[:],
                lhsT=w_codes[i][:].bitcast(FP8X4),
                lhsT_scale=w_scale[i][:],
                rhs=x_codes[:, c0:c1].bitcast(FP8X4),
                rhs_scale=x_scale[:, c0:c1],
                start=True,
                stop=True,
            )
            nc.scalar.activation(y[i][:, c0:c1], acc[:], ACT.Gelu_apprx_tanh)

        def window(i, offs, h):
            return y[i][:].indirect(offs[:, h * HALF // STRIPE : (h + 1) * HALF // STRIPE])

        def gather_weighted(dst, i, offs, weight, h):
            nc.vector.tensor_tensor(dst, window(i, offs, h), weight[:, h * HALF : (h + 1) * HALF], ALU.mult)

        def gather_plain(dst, i, h):
            nc.scalar.activation(dst, window(i, left_offs, h), ACT.Copy)

        def turn(picked, b):
            turned = bank(b, [P, 2, len(picked), P])
            for a, term in enumerate(picked):
                for c in range(2):
                    nc.tensor.transpose(turned[:, c, a, :], term[:, c * P : (c + 1) * P], ident[:])
            return turned

        def weigh(staged, turned, b0, back):
            n = turned.shape[2]
            for c in range(2):
                nc.scalar.activation(staged[:, c], turned[:, c], ACT.Copy, scale=weights[:, b0 + c : b0 + c + 1])
            for c in range(2):
                for a in range(n):
                    nc.tensor.transpose(back[c][:, a, :], staged[:, c, a, :], ident[:])

        out_rows = out_0.rearrange("(p t) v -> p t v", t=PACK)
        out_words = out_1[0].rearrange("p n t -> p (n t)").bitcast(I32)
        o_scale = sbuf("o_scale", [P, T], U8)
        sums = [sbuf(f"sums{h}", [P, PACK, HALF], F32) for h in range(2)]

        def store_sums(u, h):
            rows = slice(2 * u, 2 * u + 2)
            nc.sync.dma_start(out=out_rows[:, rows, h * HALF : (h + 1) * HALF], in_=sums[h][:, rows, :])

        def round_sums(copy, h, c0, c1):
            copy(
                out=o_bf[:, h * HALF + c0 : h * HALF + c1, :].rearrange("p (c i) t -> p c t i", i=4),
                in_=sums[h][:, :, c0:c1].rearrange("p t (c i) -> p c t i", i=4),
            )

        def quantize_out(codes, v0, v1):
            nc.vector.quantize_mx(
                out=codes.bitcast(FP8X4),
                scales=o_scale[:, v0:v1],
                in_=o_bf[:, v0:v1, :].rearrange("p v t -> p (v t)"),
            )

        round_w(nc.vector.tensor_copy, 0, 0, 2)
        for t in range(2):
            round_w(nc.vector.tensor_copy, 1, t, t + 1)
        for s in range(2):
            round_w(nc.scalar.copy, s, 2, PACK)
        for t in range(PACK):
            quantize_w(t)
        project(0, 0, HALF, 0)
        project(0, HALF, T, 1)
        for t in range(1, PACK):
            project(t, 0, T, 1 + t)

        f_left = sbuf("f_left", [P, T], F32)
        nc.vector.tensor_scalar(f_left[:], f_right[:], -1.0, 1.0, ALU.mult, ALU.add)
        rights = sbuf("rights", [P, PACK, T], F32)
        lefts = sbuf("lefts", [P, 2, HALF], F32)

        def gather_right_whole(t):
            nc.vector.tensor_tensor(rights[:, t, :], y[t][:].indirect(right_offs[:]), f_right[:], ALU.mult)

        for t in range(2):
            gather_right_whole(t)
            gather_weighted(lefts[:, t, :], t, left_offs, f_left, 0)

        for a, (t, h) in enumerate(((2, 0), (3, 0), (0, 1))):
            gather_plain(early[:, a, :], t, h)
        frac_turned = bank(2, [P, P])
        nc.tensor.transpose(frac_turned[:], f_blocks, ident[:])
        weights = sbuf("weights", [P, PACK], F32)
        nc.scalar.activation(weights[:], frac_turned[:, :PACK], ACT.Copy, scale=-1.0, bias=1.0)
        gather_plain(early[:, 3, :], 1, 1)
        back_0 = [bank(b, [P, 2, P]) for b in (5, 3)]
        turned_first = turn([early[:, 0, :], early[:, 1, :]], 0)
        turned_second = turn([early[:, 2, :], early[:, 3, :]], 1)
        weigh(sbuf("staged0", [P, 2, 2, P], F32), turned_first, 0, back_0)
        gather_plain(early[:, 1, :], 2, 1)
        turned_last = turn([early[:, 1, :]], 4)
        back_1 = bank(6, [P, 2, HALF])
        weigh(sbuf("staged1", [P, 2, 2, P], F32), turned_second, 2, [back_1[:, :, c * P : (c + 1) * P] for c in range(2)])
        left_3 = early[:, 3, :]
        gather_plain(left_3, 3, 1)
        back_2 = bank(7, [P, 1, HALF])
        weigh(sums[1][:, 3, :].rearrange("p (c a i) -> p c a i", c=2, a=1), turned_last, 2, [back_2[:, :, c * P : (c + 1) * P] for c in range(2)])
        o_bf = sbuf("staged1", [P, T, PACK], BF16)

        for t in (2, 3):
            gather_right_whole(t)
        nc.vector.tensor_tensor(sums[0][:, 0:2, :], rights[:, 0:2, :HALF], lefts[:], ALU.add)
        store_sums(0, 0)
        nc.vector.tensor_tensor(sums[0][:, 2:4, :P], back_0[0][:], rights[:, 2:4, :P], ALU.add)
        right_last, left_last = rights[:, 3, HALF:], lefts[:, 0, :]
        nc.vector.tensor_tensor(sums[0][:, 2:4, P:], back_0[1][:], rights[:, 2:4, P:HALF], ALU.add)
        store_sums(1, 0)
        for c0 in (0, P):
            round_sums(nc.scalar.copy, 0, c0, c0 + P)
        nc.gpsimd.tensor_tensor(left_last, left_3, f_left[:, HALF:], ALU.mult)
        nc.vector.tensor_tensor(sums[1][:, 0:2, :], back_1[:], rights[:, 0:2, HALF:], ALU.add)
        store_sums(0, 1)
        nc.vector.tensor_tensor(sums[1][:, 2, :], back_2[:, 0, :], rights[:, 2, HALF:], ALU.add)
        for c0 in (P, 0):
            cols = slice(c0, c0 + P)
            nc.vector.tensor_tensor(sums[1][:, 3, cols], left_last[:, cols], right_last[:, cols], ALU.add)
        store_sums(1, 1)
        round_sums(nc.scalar.copy, 1, P, HALF)
        codes = [sbuf(name, [P, HALF], U32) for name in ("codes0", "codes1")]
        quantize_out(codes[0][:], 0, HALF)
        nc.sync.dma_start(out=out_words[:, :HALF], in_=codes[0][:].bitcast(I32))
        round_sums(nc.vector.tensor_copy, 1, 0, P)
        for c0 in (P, 0):
            quantize_out(codes[1][:, c0 : c0 + P], HALF + c0, HALF + c0 + P)
        nc.sync.dma_start(out=out_words[:, HALF:], in_=codes[1][:].bitcast(I32))

        for q in range(4):
            queue = nc.scalar if q % 2 else nc.sync
            queue.dma_start(
                out=out_2[0, 4 * q : 4 * q + 4, :].bitcast(I32),
                in_=o_scale[32 * q : 32 * q + 4, :].bitcast(I32),
            )
